import numpy as np
import ml_dtypes


def mxq(x, axis, fmt="e4m3"):
    dtype, down = {"e4m3": (ml_dtypes.float8_e4m3fn, 7), "e5m2": (ml_dtypes.float8_e5m2, 14)}[fmt]
    v = np.moveaxis(np.asarray(x, np.float32).astype(ml_dtypes.bfloat16).astype(np.float64), axis, -1)
    blocks = v.reshape(v.shape[:-1] + (-1, 32))
    amax = np.abs(blocks).max(-1, keepdims=True)
    byte = np.maximum(np.where(amax > 0, np.frexp(amax)[1] - 1 + 127, 0) - down, 1)
    scale = np.exp2(byte - 127.0)
    codes = (blocks / scale).astype(np.float32).astype(dtype).astype(np.float64)
    return np.moveaxis((codes * scale).reshape(v.shape), -1, axis)


WIDE = False


def mx_kscale(k):
    if not WIDE:
        return np.ones(k)
    levels = np.array([10, -10, 5, -5, 0])
    if k % 512:
        return np.exp2(np.random.permutation(np.resize(levels, k // 32))).repeat(32)
    a = np.empty((k // 512, 16))
    for p in range(k // 512):
        a[p, :8] = np.random.permutation(np.resize(levels, 8))
        for g in range(8):
            far = levels[np.abs(levels - a[p, g]) >= 10]
            a[p, g + 8] = far[np.random.randint(len(far))]
    return np.exp2(a.ravel()).repeat(32)


def f64(x):
    return np.asarray(x).astype(np.float64)


def striped(idx):
    return np.tile(idx.reshape(-1, 16).T, (8, 1)).astype(np.uint16)


def unstriped(offs):
    return offs[:16].T.reshape(-1).astype(np.int64)


E2M1 = np.array([0.0, 0.5, 1.0, 1.5, 2.0, 3.0, 4.0, 6.0, -0.0, -0.5, -1.0, -1.5, -2.0, -3.0, -4.0, -6.0])


def pack_fp4(w):
    k, n = w.shape
    w = f64(np.asarray(w, np.float32).astype(ml_dtypes.bfloat16)).reshape(k // 32, 32, n)
    amax = np.abs(w).max(1)
    mant, ex = np.frexp(amax / 6.0)
    byte = np.clip(np.where(amax > 0, np.where(mant > 0.5, ex, ex - 1) + 127, 1), 1, 254)
    scaled = (w * np.exp2(127.0 - byte)[:, None, :]).reshape(k, n).astype(np.float32)
    c = np.ascontiguousarray(scaled.reshape(k // 512, 128, 4, n).transpose(0, 1, 3, 2)).astype(ml_dtypes.float4_e2m1fn).view(np.uint8) & 0xF
    words = (c[..., 0::2] | (c[..., 1::2] << 4)).reshape(k // 512, 128, 2 * n)
    return np.ascontiguousarray(words), np.ascontiguousarray(byte.astype(np.uint8).reshape(k // 512, 16, n))


def unpack_fp4(words, scales):
    g, _, n = scales.shape
    words = np.ascontiguousarray(words).reshape(g, 128, n, 2)
    nib = np.empty((g, 128, n, 4), np.uint8)
    nib[..., 0::2] = words & 0xF
    nib[..., 1::2] = words >> 4
    vals = E2M1[nib] * np.repeat(np.exp2(scales.astype(np.float64) - 127.0), 8, axis=1)[..., None]
    return vals.transpose(0, 1, 3, 2).reshape(g * 512, n)


def relu(v):
    return np.maximum(v, 0.0)


K, T, S, N = 1024, 1024, 512, 256
P = 2 ** 7


def setup_inputs():
    n = np.random.standard_normal
    s = mx_kscale(K)[:, None]
    packed_w1 = pack_fp4(n((K, N)) / np.sqrt(K) / s)
    return {
        "xT": (n((K, T)) * s).astype(np.float32),
        "tscale": np.tile(np.random.uniform(0.25, 2.0, T), (P, 1)).astype(np.float32),
        "cscale": np.random.uniform(0.5, 1.5, (N, 1)).astype(np.float32),
        "w1_words": packed_w1[0],
        "w1_scales": packed_w1[1],
        "offs": striped(np.random.permutation(T)[:S]),
    }


def reference(xT, tscale, cscale, w1_words, w1_scales, offs):
    xq = mxq(f64(xT)[:, unstriped(offs)], 0, "e4m3")
    y = unpack_fp4(w1_words, w1_scales).T @ xq
    tg = f64(tscale)[:1][:, unstriped(offs)]
    return relu((f64(cscale) * y) * tg)

@@ -1,0 +1,167 @@
+from contextlib import ExitStack
+
+import concourse.mybir as mybir
+from concourse.masks import make_identity
+
+K, T, S, N = 1024, 1024, 512, 256
+P = 128
+FLOPS = 2 * K * S * N
+
+F32 = mybir.dt.float32
+BF16 = mybir.dt.bfloat16
+I32 = mybir.dt.int32
+U32 = mybir.dt.uint32
+U16 = mybir.dt.uint16
+U8 = mybir.dt.uint8
+FP8X4 = mybir.dt.float8_e4m3fn_x4
+FP4X4 = mybir.dt.float4_e2m1fn_x4
+ACT = mybir.ActivationFunctionType
+ALU = mybir.AluOpType
+
+PASSES = 2
+BLOCKS = N // P
+HALF = T // 2
+PIECE = 128
+PIECES = S // PIECE
+SCALAR_COLS = {(0, 0): 0, (0, 1): 0, (3, 1): 160}
+
+
+def tile_picked_tokscale_relu_l_kernel(
+    tc, xT, tscale, cscale, w1_words, w1_scales, offs, out
+):
+    nc = tc.nc
+    with ExitStack() as ctx:
+        keep = ctx.enter_context(tc.tile_pool(name="keep", bufs=1))
+        psum = ctx.enter_context(tc.psum_pool(name="psum", bufs=1))
+
+        offsets = keep.tile([P, S // 16], U16, name="offsets")
+        x_rows = xT.rearrange("(g p u e) t -> g u p e t", g=PASSES, p=P, u=2, e=2)
+        raw = {}
+
+        def load_x(j, h):
+            raw[j, h] = keep.tile([P, 2, HALF], F32, name="raw%d_%d" % (j, h))
+            nc.sync.dma_start(out=raw[j, h][:], in_=x_rows[j // 2, j % 2][:, :, h * HALF : (h + 1) * HALF])
+
+        t_small = keep.tile([P, T // P], F32, name="t_small")
+        nc.sync.dma_start(out=t_small[:], in_=tscale[0:1, :].rearrange("o (p m) -> (o p) m", p=P))
+        c_col = keep.tile([P, BLOCKS], F32, name="c_col")
+        with nc.allow_non_contiguous_dma(reason="one channel scale a partition"):
+            nc.scalar.dma_start(out=c_col[:], in_=cscale.rearrange("(b p) o -> p (b o)", p=P))
+
+        w_words = keep.tile([P, PASSES, 2 * N], U8, name="w_words", align_bytes=64)
+        w_scales = keep.tile([P, PASSES, N], U8, name="w_scales", align_bytes=64)
+        nc.sync.dma_start(offsets[:], offs)
+        for j in range(4):
+            load_x(j, 0)
+            load_x(j, 1)
+        nc.sync.dma_start(out=w_words[:].bitcast(I32), in_=w1_words.rearrange("z p n -> p z n").bitcast(I32))
+
+        ident = keep.tile([P, P], F32, name="ident")
+        make_identity(nc, ident[:])
+        nc.gpsimd.memset(w_scales[:].bitcast(I32), 0)
+        for q in range(4):
+            nc.gpsimd.dma_start(
+                out=w_scales[32 * q : 32 * q + 4].bitcast(I32),
+                in_=w1_scales[:, 4 * q : 4 * q + 4, :].rearrange("z r n -> r z n").bitcast(I32),
+            )
+
+        t_window = keep.tile([P, T], F32, name="t_window")
+        t_view = t_window[:].rearrange("p (n h m) -> p h n m", h=2, m=4)
+        for h in range(2):
+            bank = psum.tile([P, 4, P], F32, name="t_bank%d" % h)
+            for m in range(4):
+                nc.tensor.transpose(bank[:, m, :], t_small[:, 4 * h + m : 4 * h + m + 1].to_broadcast([P, P]), ident[:])
+            nc.scalar.activation(t_view[:, h], bank[:].rearrange("p m n -> p n m"), ACT.Copy)
+        t_picked = keep.tile([P, S], F32, name="t_picked")
+        nc.vector.tensor_copy(t_picked[:], t_window[:].indirect(offsets[:]))
+
+        def cast(engine, pairs, j, h, c0, c1):
+            dst = pairs[:, 2 * (h * HALF + c0) : 2 * (h * HALF + c1)].rearrange("p (t e) -> p t e", e=2)
+            src = raw[j, h][:, :, c0:c1].rearrange("p e t -> p t e")
+            if engine == "scalar":
+                nc.scalar.activation(dst, src, ACT.Copy)
+            else:
+                nc.vector.tensor_copy(dst, src)
+
+        def make_pairs(j):
+            pairs = keep.tile([P, 2 * T], BF16, name="pairs%d" % j)
+            for h in range(2):
+                split = SCALAR_COLS.get((j, h), HALF)
+                if split > 0:
+                    cast("scalar", pairs, j, h, 0, split)
+                if split < HALF:
+                    cast("vector", pairs, j, h, split, HALF)
+            return pairs[:].bitcast(U32)
+
+        picked0 = keep.tile([P, 2 * S], U32, name="picked0")
+        for u in range(2):
+            window = make_pairs(u)
+            nc.vector.tensor_copy(picked0[:, u * S : (u + 1) * S], window.indirect(offsets[:]))
+        woven0 = keep.tile([P, 2 * S], I32, name="woven0", align_bytes=64)
+        nc.vector.tensor_copy(
+            woven0[:].rearrange("p (s u) -> p s u", u=2),
+            picked0[:].bitcast(I32).rearrange("p (u s) -> p s u", u=2),
+        )
+        codes0 = keep.tile([P, S], U32, name="codes0", align_bytes=64)
+        scales0 = keep.tile([P, S], U8, name="scales0", align_bytes=64)
+        nc.vector.quantize_mx(out=codes0[:].bitcast(FP8X4), scales=scales0[:], in_=woven0[:].bitcast(BF16))
+
+        picked1 = keep.tile([P, 2 * S], U32, name="picked1")
+        window = make_pairs(2)
+        nc.vector.tensor_copy(
+            picked1[:].rearrange("p (i u s) -> p i u s", u=2, s=PIECE)[:, :, 0, :], window.indirect(offsets[:])
+        )
+        window = make_pairs(3)
+        out_view = out.rearrange("(b p) s -> p b s", p=P)
+        cols = PIECE // 16
+
+        def gather(i):
+            nc.vector.tensor_copy(
+                picked1[:, (2 * i + 1) * PIECE : (2 * i + 2) * PIECE],
+                window.indirect(offsets[:, i * cols : (i + 1) * cols]),
+            )
+            woven = keep.tile([P, 2 * PIECE], U32, name="woven1_%d" % i, align_bytes=64)
+            nc.scalar.copy(
+                woven[:].rearrange("p (s u) -> p s u", u=2),
+                picked1[:, 2 * i * PIECE : (2 * i + 2) * PIECE].rearrange("p (u s) -> p s u", u=2),
+            )
+            return woven
+
+        def multiply(i, woven):
+            codes1 = keep.tile([P, PIECE], U32, name="codes1_%d" % i, align_bytes=64)
+            scales1 = keep.tile([P, PIECE], U8, name="scales1_%d" % i, align_bytes=64)
+            nc.vector.quantize_mx(out=codes1[:].bitcast(FP8X4), scales=scales1[:], in_=woven[:].bitcast(BF16))
+            acc = psum.tile([P, BLOCKS, PIECE], F32, name="acc%d" % i)
+            tok = slice(i * PIECE, (i + 1) * PIECE)
+            moving = ((codes0[:, tok], scales0[:, tok]), (codes1[:], scales1[:]))
+            for b in range(BLOCKS):
+                for g in range(PASSES):
+                    nc.tensor.matmul_mx(
+                        out=acc[:, b, :],
+                        lhsT=w_words[:, g, 2 * P * b : 2 * P * (b + 1)].bitcast(FP4X4),
+                        lhsT_scale=w_scales[:, g, P * b : P * (b + 1)],
+                        rhs=moving[g][0].bitcast(FP8X4),
+                        rhs_scale=moving[g][1],
+                        start=(g == 0),
+                        stop=(g == PASSES - 1),
+                    )
+            return acc
+
+        def finish(i, acc):
+            tok = slice(i * PIECE, (i + 1) * PIECE)
+            scaled = keep.tile([P, BLOCKS, PIECE], F32, name="scaled%d" % i)
+            nc.vector.tensor_tensor(scaled[:], acc[:], t_picked[:, tok].unsqueeze(1).to_broadcast([P, BLOCKS, PIECE]), ALU.mult)
+            result = keep.tile([P, BLOCKS, PIECE], F32, name="result%d" % i)
+            for b in range(BLOCKS):
+                nc.scalar.activation(result[:, b, :], scaled[:, b, :], ACT.Relu, scale=c_col[:, b : b + 1])
+            nc.sync.dma_start(out=out_view[:, :, tok], in_=result[:])
+
+        woven = {}
+        acc = {}
+        for step in range(PIECES + 2):
+            if step < PIECES:
+                woven[step] = gather(step)
+            if 0 <= step - 1 < PIECES:
+                acc[step - 1] = multiply(step - 1, woven[step - 1])
+            if 0 <= step - 2 < PIECES:
+                finish(step - 2, acc[step - 2])

@@ -23,7 +23,9 @@ BLOCKS = N // P
 HALF = T // 2
 PIECE = 128
 PIECES = S // PIECE
-SCALAR_COLS = {(0, 0): 0, (0, 1): 0, (3, 1): 160}
+LAST_SPLIT = 160
+SCALAR_COLS = {(0, 0): 0, (0, 1): 0, (3, 1): LAST_SPLIT}
+OVERLAP_START = HALF + LAST_SPLIT
 
 
 def tile_picked_tokscale_relu_l_kernel(
@@ -42,7 +44,7 @@ def tile_picked_tokscale_relu_l_kernel(
             raw[j, h] = keep.tile([P, 2, HALF], F32, name="raw%d_%d" % (j, h))
             nc.sync.dma_start(out=raw[j, h][:], in_=x_rows[j // 2, j % 2][:, :, h * HALF : (h + 1) * HALF])
 
-        t_small = keep.tile([P, T // P], F32, name="t_small")
+        t_small = keep.tile([P, T // P], F32, name="t_small", tag="pairs1")
         nc.sync.dma_start(out=t_small[:], in_=tscale[0:1, :].rearrange("o (p m) -> (o p) m", p=P))
         c_col = keep.tile([P, BLOCKS], F32, name="c_col")
         with nc.allow_non_contiguous_dma(reason="one channel scale a partition"):
@@ -51,24 +53,25 @@ def tile_picked_tokscale_relu_l_kernel(
         w_words = keep.tile([P, PASSES, 2 * N], U8, name="w_words", align_bytes=64)
         w_scales = keep.tile([P, PASSES, N], U8, name="w_scales", align_bytes=64)
         nc.sync.dma_start(offsets[:], offs)
+        nc.vector.memset(w_scales[:].bitcast(I32), 0)
         for j in range(4):
+            if j == 3:
+                for q in range(4):
+                    nc.sync.dma_start(
+                        out=w_scales[32 * q : 32 * q + 4].bitcast(I32),
+                        in_=w1_scales[:, 4 * q : 4 * q + 4, :].rearrange("z r n -> r z n").bitcast(I32),
+                    )
             load_x(j, 0)
             load_x(j, 1)
         nc.sync.dma_start(out=w_words[:].bitcast(I32), in_=w1_words.rearrange("z p n -> p z n").bitcast(I32))
 
-        ident = keep.tile([P, P], F32, name="ident")
+        ident = keep.tile([P, P], F32, name="ident", tag="pairs2")
         make_identity(nc, ident[:])
-        nc.gpsimd.memset(w_scales[:].bitcast(I32), 0)
-        for q in range(4):
-            nc.gpsimd.dma_start(
-                out=w_scales[32 * q : 32 * q + 4].bitcast(I32),
-                in_=w1_scales[:, 4 * q : 4 * q + 4, :].rearrange("z r n -> r z n").bitcast(I32),
-            )
 
         t_window = keep.tile([P, T], F32, name="t_window")
         t_view = t_window[:].rearrange("p (n h m) -> p h n m", h=2, m=4)
         for h in range(2):
-            bank = psum.tile([P, 4, P], F32, name="t_bank%d" % h)
+            bank = psum.tile([P, 4, P], F32, name="t_bank%d" % h, tag="bank%d" % (6 + h))
             for m in range(4):
                 nc.tensor.transpose(bank[:, m, :], t_small[:, 4 * h + m : 4 * h + m + 1].to_broadcast([P, P]), ident[:])
             nc.scalar.activation(t_view[:, h], bank[:].rearrange("p m n -> p n m"), ACT.Copy)
@@ -83,85 +86,98 @@ def tile_picked_tokscale_relu_l_kernel(
             else:
                 nc.vector.tensor_copy(dst, src)
 
-        def make_pairs(j):
-            pairs = keep.tile([P, 2 * T], BF16, name="pairs%d" % j)
+        def make_pairs(j, pairs):
             for h in range(2):
                 split = SCALAR_COLS.get((j, h), HALF)
                 if split > 0:
                     cast("scalar", pairs, j, h, 0, split)
                 if split < HALF:
                     cast("vector", pairs, j, h, split, HALF)
-            return pairs[:].bitcast(U32)
+            return pairs.bitcast(U32)
 
+        half = S // 2
         picked0 = keep.tile([P, 2 * S], U32, name="picked0")
-        for u in range(2):
-            window = make_pairs(u)
-            nc.vector.tensor_copy(picked0[:, u * S : (u + 1) * S], window.indirect(offsets[:]))
-        woven0 = keep.tile([P, 2 * S], I32, name="woven0", align_bytes=64)
+        pairs = keep.tile([P, 2 * T], BF16, name="pairs0", tag="pairs0")
+        window = make_pairs(0, pairs[:])
         nc.vector.tensor_copy(
-            woven0[:].rearrange("p (s u) -> p s u", u=2),
-            picked0[:].bitcast(I32).rearrange("p (u s) -> p s u", u=2),
+            picked0[:].rearrange("p (i u s) -> p i u s", u=2, s=half)[:, :, 0, :], window.indirect(offsets[:])
         )
+        pairs = keep.tile([P, 2 * T], BF16, name="pairs1", tag="pairs1")
+        window = make_pairs(1, pairs[:])
         codes0 = keep.tile([P, S], U32, name="codes0", align_bytes=64)
         scales0 = keep.tile([P, S], U8, name="scales0", align_bytes=64)
-        nc.vector.quantize_mx(out=codes0[:].bitcast(FP8X4), scales=scales0[:], in_=woven0[:].bitcast(BF16))
+        woven0 = keep.tile([P, 2 * S], I32, name="woven0", align_bytes=64)
+        for i in range(2):
+            nc.vector.tensor_copy(
+                picked0[:, (2 * i + 1) * half : (2 * i + 2) * half],
+                window.indirect(offsets[:, i * half // 16 : (i + 1) * half // 16]),
+            )
+        for i in range(2):
+            nc.vector.tensor_copy(
+                woven0[:, i * S : (i + 1) * S].rearrange("p (s u) -> p s u", u=2),
+                picked0[:, i * S : (i + 1) * S].bitcast(I32).rearrange("p (u s) -> p s u", u=2),
+            )
+        for i in range(2):
+            nc.vector.quantize_mx(
+                out=codes0[:, i * half : (i + 1) * half].bitcast(FP8X4),
+                scales=scales0[:, i * half : (i + 1) * half],
+                in_=woven0[:, i * S : (i + 1) * S].bitcast(BF16),
+            )
+
+        acc = {}
+
+        def product(i, b, g, codes, scales):
+            nc.tensor.matmul_mx(
+                out=acc[i, b][:],
+                lhsT=w_words[:, g, 2 * P * b : 2 * P * (b + 1)].bitcast(FP4X4),
+                lhsT_scale=w_scales[:, g, P * b : P * (b + 1)],
+                rhs=codes.bitcast(FP8X4),
+                rhs_scale=scales,
+                start=(g == 0),
+                stop=(g == PASSES - 1),
+            )
+
+        for i in range(PIECES):
+            tok = slice(i * PIECE, (i + 1) * PIECE)
+            for b in range(BLOCKS):
+                acc[i, b] = psum.tile([P, PIECE], F32, name="acc%d_%d" % (i, b), tag="bank%d" % (2 * i + b))
+                product(i, b, 0, codes0[:, tok], scales0[:, tok])
 
         picked1 = keep.tile([P, 2 * S], U32, name="picked1")
-        window = make_pairs(2)
+        pairs = keep.tile([P, 2 * (OVERLAP_START + T)], BF16, name="pairs2", tag="pairs2")
+        window = make_pairs(2, pairs[:, 2 * OVERLAP_START :])
         nc.vector.tensor_copy(
             picked1[:].rearrange("p (i u s) -> p i u s", u=2, s=PIECE)[:, :, 0, :], window.indirect(offsets[:])
         )
-        window = make_pairs(3)
+        window = make_pairs(3, pairs[:, : 2 * T])
         out_view = out.rearrange("(b p) s -> p b s", p=P)
         cols = PIECE // 16
-
-        def gather(i):
+        woven = {}
+        for i in range(PIECES):
             nc.vector.tensor_copy(
                 picked1[:, (2 * i + 1) * PIECE : (2 * i + 2) * PIECE],
                 window.indirect(offsets[:, i * cols : (i + 1) * cols]),
             )
-            woven = keep.tile([P, 2 * PIECE], U32, name="woven1_%d" % i, align_bytes=64)
+            woven[i] = keep.tile([P, 2 * PIECE], U32, name="woven1_%d" % i, tag="stage%d" % i, align_bytes=64)
             nc.scalar.copy(
-                woven[:].rearrange("p (s u) -> p s u", u=2),
+                woven[i][:].rearrange("p (s u) -> p s u", u=2),
                 picked1[:, 2 * i * PIECE : (2 * i + 2) * PIECE].rearrange("p (u s) -> p s u", u=2),
             )
-            return woven
-
-        def multiply(i, woven):
+        for i in range(PIECES):
             codes1 = keep.tile([P, PIECE], U32, name="codes1_%d" % i, align_bytes=64)
             scales1 = keep.tile([P, PIECE], U8, name="scales1_%d" % i, align_bytes=64)
-            nc.vector.quantize_mx(out=codes1[:].bitcast(FP8X4), scales=scales1[:], in_=woven[:].bitcast(BF16))
-            acc = psum.tile([P, BLOCKS, PIECE], F32, name="acc%d" % i)
-            tok = slice(i * PIECE, (i + 1) * PIECE)
-            moving = ((codes0[:, tok], scales0[:, tok]), (codes1[:], scales1[:]))
+            nc.vector.quantize_mx(out=codes1[:].bitcast(FP8X4), scales=scales1[:], in_=woven[i][:].bitcast(BF16))
             for b in range(BLOCKS):
-                for g in range(PASSES):
-                    nc.tensor.matmul_mx(
-                        out=acc[:, b, :],
-                        lhsT=w_words[:, g, 2 * P * b : 2 * P * (b + 1)].bitcast(FP4X4),
-                        lhsT_scale=w_scales[:, g, P * b : P * (b + 1)],
-                        rhs=moving[g][0].bitcast(FP8X4),
-                        rhs_scale=moving[g][1],
-                        start=(g == 0),
-                        stop=(g == PASSES - 1),
-                    )
-            return acc
-
-        def finish(i, acc):
+                product(i, b, 1, codes1[:], scales1[:])
+        for i in range(PIECES):
             tok = slice(i * PIECE, (i + 1) * PIECE)
-            scaled = keep.tile([P, BLOCKS, PIECE], F32, name="scaled%d" % i)
-            nc.vector.tensor_tensor(scaled[:], acc[:], t_picked[:, tok].unsqueeze(1).to_broadcast([P, BLOCKS, PIECE]), ALU.mult)
+            scaled = keep.tile(
+                [P, BLOCKS, PIECE], F32, name="scaled%d" % i, tag="stage%d" % (PIECES - 1 - i), align_bytes=64
+            )
+            for b in range(BLOCKS):
+                nc.vector.scalar_tensor_tensor(
+                    scaled[:, b, :], acc[i, b][:], c_col[:, b : b + 1], t_picked[:, tok], ALU.mult, ALU.mult
+                )
             result = keep.tile([P, BLOCKS, PIECE], F32, name="result%d" % i)
-            for b in range(BLOCKS):
-                nc.scalar.activation(result[:, b, :], scaled[:, b, :], ACT.Relu, scale=c_col[:, b : b + 1])
+            nc.scalar.activation(result[:], scaled[:], ACT.Relu)
             nc.sync.dma_start(out=out_view[:, :, tok], in_=result[:])
-
-        woven = {}
-        acc = {}
-        for step in range(PIECES + 2):
-            if step < PIECES:
-                woven[step] = gather(step)
-            if 0 <= step - 1 < PIECES:
-                acc[step - 1] = multiply(step - 1, woven[step - 1])
-            if 0 <= step - 2 < PIECES:
-                finish(step - 2, acc[step - 2])

@@ -23,9 +23,8 @@ BLOCKS = N // P
 HALF = T // 2
 PIECE = 128
 PIECES = S // PIECE
-LAST_SPLIT = 160
-SCALAR_COLS = {(0, 0): 0, (0, 1): 0, (3, 1): LAST_SPLIT}
-OVERLAP_START = HALF + LAST_SPLIT
+SCALAR_COLS = {(0, 0): 0, (0, 1): 0, (1, 1): 288, (3, 1): 288}
+OVERLAP_START = T
 
 
 def tile_picked_tokscale_relu_l_kernel(
@@ -52,17 +51,17 @@ def tile_picked_tokscale_relu_l_kernel(
 
         w_words = keep.tile([P, PASSES, 2 * N], U8, name="w_words", align_bytes=64)
         w_scales = keep.tile([P, PASSES, N], U8, name="w_scales", align_bytes=64)
-        nc.sync.dma_start(offsets[:], offs)
         nc.vector.memset(w_scales[:].bitcast(I32), 0)
         for j in range(4):
-            if j == 3:
-                for q in range(4):
-                    nc.sync.dma_start(
-                        out=w_scales[32 * q : 32 * q + 4].bitcast(I32),
-                        in_=w1_scales[:, 4 * q : 4 * q + 4, :].rearrange("z r n -> r z n").bitcast(I32),
-                    )
             load_x(j, 0)
+            if j == 0:
+                nc.sync.dma_start(offsets[:], offs)
             load_x(j, 1)
+        for q in range(4):
+            nc.sync.dma_start(
+                out=w_scales[32 * q : 32 * q + 4].bitcast(I32),
+                in_=w1_scales[:, 4 * q : 4 * q + 4, :].rearrange("z r n -> r z n").bitcast(I32),
+            )
         nc.sync.dma_start(out=w_words[:].bitcast(I32), in_=w1_words.rearrange("z p n -> p z n").bitcast(I32))
 
         ident = keep.tile([P, P], F32, name="ident", tag="pairs2")
@@ -83,8 +82,10 @@ def tile_picked_tokscale_relu_l_kernel(
             src = raw[j, h][:, :, c0:c1].rearrange("p e t -> p t e")
             if engine == "scalar":
                 nc.scalar.activation(dst, src, ACT.Copy)
-            else:
+            elif engine == "vector":
                 nc.vector.tensor_copy(dst, src)
+            else:
+                nc.gpsimd.tensor_scalar(dst, src, 1.0, 0.0, ALU.mult, ALU.add)
 
         def make_pairs(j, pairs):
             for h in range(2):
@@ -92,7 +93,7 @@ def tile_picked_tokscale_relu_l_kernel(
                 if split > 0:
                     cast("scalar", pairs, j, h, 0, split)
                 if split < HALF:
-                    cast("vector", pairs, j, h, split, HALF)
+                    cast("vector" if j == 0 else "gpsimd", pairs, j, h, split, HALF)
             return pairs.bitcast(U32)
 
         half = S // 2
@@ -172,12 +173,17 @@ def tile_picked_tokscale_relu_l_kernel(
         for i in range(PIECES):
             tok = slice(i * PIECE, (i + 1) * PIECE)
             scaled = keep.tile(
-                [P, BLOCKS, PIECE], F32, name="scaled%d" % i, tag="stage%d" % (PIECES - 1 - i), align_bytes=64
+                [P, BLOCKS, PIECE], F32, name="scaled%d" % i, tag="stage%d" % ((i + 2) % PIECES), align_bytes=64
             )
             for b in range(BLOCKS):
                 nc.vector.scalar_tensor_tensor(
                     scaled[:, b, :], acc[i, b][:], c_col[:, b : b + 1], t_picked[:, tok], ALU.mult, ALU.mult
                 )
             result = keep.tile([P, BLOCKS, PIECE], F32, name="result%d" % i)
-            nc.scalar.activation(result[:], scaled[:], ACT.Relu)
-            nc.sync.dma_start(out=out_view[:, :, tok], in_=result[:])
+            if i < PIECES - 1:
+                nc.scalar.activation(result[:], scaled[:], ACT.Relu)
+                nc.sync.dma_start(out=out_view[:, :, tok], in_=result[:])
+            else:
+                for b, queue in enumerate((nc.sync, nc.scalar)):
+                    nc.scalar.activation(result[:, b, :], scaled[:, b, :], ACT.Relu)
+                    queue.dma_start(out=out_view[:, b, tok], in_=result[:, b, :])

@@ -23,7 +23,7 @@ BLOCKS = N // P
 HALF = T // 2
 PIECE = 128
 PIECES = S // PIECE
-SCALAR_COLS = {(0, 0): 0, (0, 1): 0, (1, 1): 288, (3, 1): 288}
+SCALAR_COLS = {(0, 0): 0, (0, 1): 0, (3, 1): 288}
 OVERLAP_START = T
 
 
@@ -46,26 +46,26 @@ def tile_picked_tokscale_relu_l_kernel(
         t_small = keep.tile([P, T // P], F32, name="t_small", tag="pairs1")
         nc.sync.dma_start(out=t_small[:], in_=tscale[0:1, :].rearrange("o (p m) -> (o p) m", p=P))
         c_col = keep.tile([P, BLOCKS], F32, name="c_col")
-        with nc.allow_non_contiguous_dma(reason="one channel scale a partition"):
-            nc.scalar.dma_start(out=c_col[:], in_=cscale.rearrange("(b p) o -> p (b o)", p=P))
 
         w_words = keep.tile([P, PASSES, 2 * N], U8, name="w_words", align_bytes=64)
         w_scales = keep.tile([P, PASSES, N], U8, name="w_scales", align_bytes=64)
-        nc.vector.memset(w_scales[:].bitcast(I32), 0)
         for j in range(4):
             load_x(j, 0)
             if j == 0:
                 nc.sync.dma_start(offsets[:], offs)
             load_x(j, 1)
-        for q in range(4):
-            nc.sync.dma_start(
-                out=w_scales[32 * q : 32 * q + 4].bitcast(I32),
-                in_=w1_scales[:, 4 * q : 4 * q + 4, :].rearrange("z r n -> r z n").bitcast(I32),
-            )
         nc.sync.dma_start(out=w_words[:].bitcast(I32), in_=w1_words.rearrange("z p n -> p z n").bitcast(I32))
+        with nc.allow_non_contiguous_dma(reason="one channel scale a partition"):
+            nc.sync.dma_start(out=c_col[:], in_=cscale.rearrange("(b p) o -> p (b o)", p=P))
 
         ident = keep.tile([P, P], F32, name="ident", tag="pairs2")
         make_identity(nc, ident[:])
+        nc.gpsimd.memset(w_scales[:].bitcast(I32), 0)
+        for q in range(4):
+            nc.gpsimd.dma_start(
+                out=w_scales[32 * q : 32 * q + 4].bitcast(I32),
+                in_=w1_scales[:, 4 * q : 4 * q + 4, :].rearrange("z r n -> r z n").bitcast(I32),
+            )
 
         t_window = keep.tile([P, T], F32, name="t_window")
         t_view = t_window[:].rearrange("p (n h m) -> p h n m", h=2, m=4)

@@ -23,7 +23,8 @@ BLOCKS = N // P
 HALF = T // 2
 PIECE = 128
 PIECES = S // PIECE
-SCALAR_COLS = {(0, 0): 0, (0, 1): 0, (3, 1): 288}
+CHUNKS = {0: (512, 512), 1: (512, 512), 2: (512, 512), 3: (512, 256, 256)}
+SCALAR_COLS = {(0, 0): 0, (0, 1): 0, (3, 1): 64, (3, 2): 152}
 OVERLAP_START = T
 
 
@@ -40,11 +41,12 @@ def tile_picked_tokscale_relu_l_kernel(
         raw = {}
 
         def load_x(j, h):
-            raw[j, h] = keep.tile([P, 2, HALF], F32, name="raw%d_%d" % (j, h))
-            nc.sync.dma_start(out=raw[j, h][:], in_=x_rows[j // 2, j % 2][:, :, h * HALF : (h + 1) * HALF])
+            first = sum(CHUNKS[j][:h])
+            raw[j, h] = keep.tile([P, 2, CHUNKS[j][h]], F32, name="raw%d_%d" % (j, h))
+            nc.sync.dma_start(out=raw[j, h][:], in_=x_rows[j // 2, j % 2][:, :, first : first + CHUNKS[j][h]])
 
         t_small = keep.tile([P, T // P], F32, name="t_small", tag="pairs1")
-        nc.sync.dma_start(out=t_small[:], in_=tscale[0:1, :].rearrange("o (p m) -> (o p) m", p=P))
+        nc.scalar.dma_start(out=t_small[:], in_=tscale[0:1, :].rearrange("o (p m) -> (o p) m", p=P))
         c_col = keep.tile([P, BLOCKS], F32, name="c_col")
 
         w_words = keep.tile([P, PASSES, 2 * N], U8, name="w_words", align_bytes=64)
@@ -53,7 +55,8 @@ def tile_picked_tokscale_relu_l_kernel(
             load_x(j, 0)
             if j == 0:
                 nc.sync.dma_start(offsets[:], offs)
-            load_x(j, 1)
+            for h in range(1, len(CHUNKS[j])):
+                load_x(j, h)
         nc.sync.dma_start(out=w_words[:].bitcast(I32), in_=w1_words.rearrange("z p n -> p z n").bitcast(I32))
         with nc.allow_non_contiguous_dma(reason="one channel scale a partition"):
             nc.sync.dma_start(out=c_col[:], in_=cscale.rearrange("(b p) o -> p (b o)", p=P))
@@ -78,7 +81,8 @@ def tile_picked_tokscale_relu_l_kernel(
         nc.vector.tensor_copy(t_picked[:], t_window[:].indirect(offsets[:]))
 
         def cast(engine, pairs, j, h, c0, c1):
-            dst = pairs[:, 2 * (h * HALF + c0) : 2 * (h * HALF + c1)].rearrange("p (t e) -> p t e", e=2)
+            first = sum(CHUNKS[j][:h])
+            dst = pairs[:, 2 * (first + c0) : 2 * (first + c1)].rearrange("p (t e) -> p t e", e=2)
             src = raw[j, h][:, :, c0:c1].rearrange("p e t -> p t e")
             if engine == "scalar":
                 nc.scalar.activation(dst, src, ACT.Copy)
@@ -88,12 +92,12 @@ def tile_picked_tokscale_relu_l_kernel(
                 nc.gpsimd.tensor_scalar(dst, src, 1.0, 0.0, ALU.mult, ALU.add)
 
         def make_pairs(j, pairs):
-            for h in range(2):
-                split = SCALAR_COLS.get((j, h), HALF)
+            for h, width in enumerate(CHUNKS[j]):
+                split = SCALAR_COLS.get((j, h), width)
                 if split > 0:
                     cast("scalar", pairs, j, h, 0, split)
-                if split < HALF:
-                    cast("vector" if j == 0 else "gpsimd", pairs, j, h, split, HALF)
+                if split < width:
+                    cast("vector" if j == 0 else "gpsimd", pairs, j, h, split, width)
             return pairs.bitcast(U32)
 
         half = S // 2

@@ -24,7 +24,7 @@ HALF = T // 2
 PIECE = 128
 PIECES = S // PIECE
 CHUNKS = {0: (512, 512), 1: (512, 512), 2: (512, 512), 3: (512, 256, 256)}
-SCALAR_COLS = {(0, 0): 0, (0, 1): 0, (3, 1): 64, (3, 2): 152}
+SCALAR_COLS = {(0, 0): 0, (0, 1): 0, (3, 0): 320, (3, 1): 128, (3, 2): 144}
 OVERLAP_START = T
 
 

@@ -24,7 +24,7 @@ HALF = T // 2
 PIECE = 128
 PIECES = S // PIECE
 CHUNKS = {0: (512, 512), 1: (512, 512), 2: (512, 512), 3: (512, 256, 256)}
-SCALAR_COLS = {(0, 0): 0, (0, 1): 0, (3, 0): 320, (3, 1): 128, (3, 2): 144}
+SCALAR_COLS = {(0, 0): 0, (0, 1): 0, (1, 1): 320, (3, 0): 320, (3, 1): 128, (3, 2): 144}
 OVERLAP_START = T
 
 
@@ -51,24 +51,25 @@ def tile_picked_tokscale_relu_l_kernel(
 
         w_words = keep.tile([P, PASSES, 2 * N], U8, name="w_words", align_bytes=64)
         w_scales = keep.tile([P, PASSES, N], U8, name="w_scales", align_bytes=64)
+        nc.gpsimd.memset(w_scales[:].bitcast(I32), 0)
         for j in range(4):
             load_x(j, 0)
             if j == 0:
                 nc.sync.dma_start(offsets[:], offs)
             for h in range(1, len(CHUNKS[j])):
                 load_x(j, h)
+            if j == 1:
+                for q in range(4):
+                    nc.sync.dma_start(
+                        out=w_scales[32 * q : 32 * q + 4].bitcast(I32),
+                        in_=w1_scales[:, 4 * q : 4 * q + 4, :].rearrange("z r n -> r z n").bitcast(I32),
+                    )
         nc.sync.dma_start(out=w_words[:].bitcast(I32), in_=w1_words.rearrange("z p n -> p z n").bitcast(I32))
         with nc.allow_non_contiguous_dma(reason="one channel scale a partition"):
             nc.sync.dma_start(out=c_col[:], in_=cscale.rearrange("(b p) o -> p (b o)", p=P))
 
         ident = keep.tile([P, P], F32, name="ident", tag="pairs2")
         make_identity(nc, ident[:])
-        nc.gpsimd.memset(w_scales[:].bitcast(I32), 0)
-        for q in range(4):
-            nc.gpsimd.dma_start(
-                out=w_scales[32 * q : 32 * q + 4].bitcast(I32),
-                in_=w1_scales[:, 4 * q : 4 * q + 4, :].rearrange("z r n -> r z n").bitcast(I32),
-            )
 
         t_window = keep.tile([P, T], F32, name="t_window")
         t_view = t_window[:].rearrange("p (n h m) -> p h n m", h=2, m=4)

@@ -37,20 +37,24 @@ def tile_picked_tokscale_relu_l_kernel(
         psum = ctx.enter_context(tc.psum_pool(name="psum", bufs=1))
 
         offsets = keep.tile([P, S // 16], U16, name="offsets")
+
+        def aligned(shape, dtype, name, tag=None):
+            return keep.tile(shape, dtype, name=name, tag=tag or name, align_bytes=256)
+
         x_rows = xT.rearrange("(g p u e) t -> g u p e t", g=PASSES, p=P, u=2, e=2)
         raw = {}
 
         def load_x(j, h):
             first = sum(CHUNKS[j][:h])
-            raw[j, h] = keep.tile([P, 2, CHUNKS[j][h]], F32, name="raw%d_%d" % (j, h))
+            raw[j, h] = aligned([P, 2, CHUNKS[j][h]], F32, name="raw%d_%d" % (j, h))
             nc.sync.dma_start(out=raw[j, h][:], in_=x_rows[j // 2, j % 2][:, :, first : first + CHUNKS[j][h]])
 
-        t_small = keep.tile([P, T // P], F32, name="t_small", tag="pairs1")
+        t_small = aligned([P, T // P], F32, name="t_small", tag="pairs1")
         nc.scalar.dma_start(out=t_small[:], in_=tscale[0:1, :].rearrange("o (p m) -> (o p) m", p=P))
-        c_col = keep.tile([P, BLOCKS], F32, name="c_col")
+        c_col = aligned([P, BLOCKS], F32, name="c_col")
 
-        w_words = keep.tile([P, PASSES, 2 * N], U8, name="w_words", align_bytes=64)
-        w_scales = keep.tile([P, PASSES, N], U8, name="w_scales", align_bytes=64)
+        w_words = aligned([P, PASSES, 2 * N], U8, name="w_words")
+        w_scales = aligned([P, PASSES, N], U8, name="w_scales")
         nc.gpsimd.memset(w_scales[:].bitcast(I32), 0)
         for j in range(4):
             load_x(j, 0)
@@ -68,17 +72,17 @@ def tile_picked_tokscale_relu_l_kernel(
         with nc.allow_non_contiguous_dma(reason="one channel scale a partition"):
             nc.sync.dma_start(out=c_col[:], in_=cscale.rearrange("(b p) o -> p (b o)", p=P))
 
-        ident = keep.tile([P, P], F32, name="ident", tag="pairs2")
+        ident = aligned([P, P], F32, name="ident", tag="pairs2")
         make_identity(nc, ident[:])
 
-        t_window = keep.tile([P, T], F32, name="t_window")
+        t_window = aligned([P, T], F32, name="t_window")
         t_view = t_window[:].rearrange("p (n h m) -> p h n m", h=2, m=4)
         for h in range(2):
             bank = psum.tile([P, 4, P], F32, name="t_bank%d" % h, tag="bank%d" % (6 + h))
             for m in range(4):
                 nc.tensor.transpose(bank[:, m, :], t_small[:, 4 * h + m : 4 * h + m + 1].to_broadcast([P, P]), ident[:])
             nc.scalar.activation(t_view[:, h], bank[:].rearrange("p m n -> p n m"), ACT.Copy)
-        t_picked = keep.tile([P, S], F32, name="t_picked")
+        t_picked = aligned([P, S], F32, name="t_picked")
         nc.vector.tensor_copy(t_picked[:], t_window[:].indirect(offsets[:]))
 
         def cast(engine, pairs, j, h, c0, c1):
@@ -102,17 +106,17 @@ def tile_picked_tokscale_relu_l_kernel(
             return pairs.bitcast(U32)
 
         half = S // 2
-        picked0 = keep.tile([P, 2 * S], U32, name="picked0")
-        pairs = keep.tile([P, 2 * T], BF16, name="pairs0", tag="pairs0")
+        picked0 = aligned([P, 2 * S], U32, name="picked0")
+        pairs = aligned([P, 2 * T], BF16, name="pairs0", tag="pairs0")
         window = make_pairs(0, pairs[:])
         nc.vector.tensor_copy(
             picked0[:].rearrange("p (i u s) -> p i u s", u=2, s=half)[:, :, 0, :], window.indirect(offsets[:])
         )
-        pairs = keep.tile([P, 2 * T], BF16, name="pairs1", tag="pairs1")
+        pairs = aligned([P, 2 * T], BF16, name="pairs1", tag="pairs1")
         window = make_pairs(1, pairs[:])
-        codes0 = keep.tile([P, S], U32, name="codes0", align_bytes=64)
-        scales0 = keep.tile([P, S], U8, name="scales0", align_bytes=64)
-        woven0 = keep.tile([P, 2 * S], I32, name="woven0", align_bytes=64)
+        codes0 = aligned([P, S], U32, name="codes0")
+        scales0 = aligned([P, S], U8, name="scales0")
+        woven0 = aligned([P, 2 * S], I32, name="woven0")
         for i in range(2):
             nc.vector.tensor_copy(
                 picked0[:, (2 * i + 1) * half : (2 * i + 2) * half],
@@ -149,8 +153,8 @@ def tile_picked_tokscale_relu_l_kernel(
                 acc[i, b] = psum.tile([P, PIECE], F32, name="acc%d_%d" % (i, b), tag="bank%d" % (2 * i + b))
                 product(i, b, 0, codes0[:, tok], scales0[:, tok])
 
-        picked1 = keep.tile([P, 2 * S], U32, name="picked1")
-        pairs = keep.tile([P, 2 * (OVERLAP_START + T)], BF16, name="pairs2", tag="pairs2")
+        picked1 = aligned([P, 2 * S], U32, name="picked1")
+        pairs = aligned([P, 2 * (OVERLAP_START + T)], BF16, name="pairs2", tag="pairs2")
         window = make_pairs(2, pairs[:, 2 * OVERLAP_START :])
         nc.vector.tensor_copy(
             picked1[:].rearrange("p (i u s) -> p i u s", u=2, s=PIECE)[:, :, 0, :], window.indirect(offsets[:])
@@ -164,27 +168,27 @@ def tile_picked_tokscale_relu_l_kernel(
                 picked1[:, (2 * i + 1) * PIECE : (2 * i + 2) * PIECE],
                 window.indirect(offsets[:, i * cols : (i + 1) * cols]),
             )
-            woven[i] = keep.tile([P, 2 * PIECE], U32, name="woven1_%d" % i, tag="stage%d" % i, align_bytes=64)
+            woven[i] = aligned([P, 2 * PIECE], U32, name="woven1_%d" % i, tag="stage%d" % i)
             nc.scalar.copy(
                 woven[i][:].rearrange("p (s u) -> p s u", u=2),
                 picked1[:, 2 * i * PIECE : (2 * i + 2) * PIECE].rearrange("p (u s) -> p s u", u=2),
             )
         for i in range(PIECES):
-            codes1 = keep.tile([P, PIECE], U32, name="codes1_%d" % i, align_bytes=64)
-            scales1 = keep.tile([P, PIECE], U8, name="scales1_%d" % i, align_bytes=64)
+            codes1 = aligned([P, PIECE], U32, name="codes1_%d" % i)
+            scales1 = aligned([P, PIECE], U8, name="scales1_%d" % i)
             nc.vector.quantize_mx(out=codes1[:].bitcast(FP8X4), scales=scales1[:], in_=woven[i][:].bitcast(BF16))
             for b in range(BLOCKS):
                 product(i, b, 1, codes1[:], scales1[:])
         for i in range(PIECES):
             tok = slice(i * PIECE, (i + 1) * PIECE)
-            scaled = keep.tile(
-                [P, BLOCKS, PIECE], F32, name="scaled%d" % i, tag="stage%d" % ((i + 2) % PIECES), align_bytes=64
+            scaled = aligned(
+                [P, BLOCKS, PIECE], F32, name="scaled%d" % i, tag="stage%d" % ((i + 2) % PIECES)
             )
             for b in range(BLOCKS):
                 nc.vector.scalar_tensor_tensor(
                     scaled[:, b, :], acc[i, b][:], c_col[:, b : b + 1], t_picked[:, tok], ALU.mult, ALU.mult
                 )
-            result = keep.tile([P, BLOCKS, PIECE], F32, name="result%d" % i)
+            result = aligned([P, BLOCKS, PIECE], F32, name="result%d" % i)
             if i < PIECES - 1:
                 nc.scalar.activation(result[:], scaled[:], ACT.Relu)
                 nc.sync.dma_start(out=out_view[:, :, tok], in_=result[:])

@@ -189,10 +189,15 @@ def tile_picked_tokscale_relu_l_kernel(
                     scaled[:, b, :], acc[i, b][:], c_col[:, b : b + 1], t_picked[:, tok], ALU.mult, ALU.mult
                 )
             result = aligned([P, BLOCKS, PIECE], F32, name="result%d" % i)
-            if i < PIECES - 1:
-                nc.scalar.activation(result[:], scaled[:], ACT.Relu)
-                nc.sync.dma_start(out=out_view[:, :, tok], in_=result[:])
-            else:
-                for b, queue in enumerate((nc.sync, nc.scalar)):
+            if i == 0:
+                for b in range(BLOCKS):
                     nc.scalar.activation(result[:, b, :], scaled[:, b, :], ACT.Relu)
-                    queue.dma_start(out=out_view[:, b, tok], in_=result[:, b, :])
+                    nc.sync.dma_start(out=out_view[:, b, tok], in_=result[:, b, :])
+            elif i < PIECES - 1:
+                nc.scalar.activation(result[:], scaled[:], ACT.Relu)
+                queue = nc.scalar if i == PIECES - 2 else nc.sync
+                queue.dma_start(out=out_view[:, :, tok], in_=result[:])
+            else:
+                for b in range(BLOCKS):
+                    nc.vector.tensor_scalar(result[:, b, :], scaled[:, b, :], 0.0, None, ALU.max)
+                nc.sync.dma_start(out=out_view[:, :, tok], in_=result[:])

@@ -179,25 +179,26 @@ def tile_picked_tokscale_relu_l_kernel(
             nc.vector.quantize_mx(out=codes1[:].bitcast(FP8X4), scales=scales1[:], in_=woven[i][:].bitcast(BF16))
             for b in range(BLOCKS):
                 product(i, b, 1, codes1[:], scales1[:])
-        for i in range(PIECES):
-            tok = slice(i * PIECE, (i + 1) * PIECE)
-            scaled = aligned(
-                [P, BLOCKS, PIECE], F32, name="scaled%d" % i, tag="stage%d" % ((i + 2) % PIECES)
-            )
+        for pair in range(2):
             for b in range(BLOCKS):
-                nc.vector.scalar_tensor_tensor(
-                    scaled[:, b, :], acc[i, b][:], c_col[:, b : b + 1], t_picked[:, tok], ALU.mult, ALU.mult
+                last = pair == 1 and b == BLOCKS - 1
+                scaled = aligned(
+                    [P, 2, PIECE], F32, name="scaled%d_%d" % (pair, b), tag="stage%d" % ((2 * pair + b + 2) % PIECES)
                 )
-            result = aligned([P, BLOCKS, PIECE], F32, name="result%d" % i)
-            if i == 0:
-                for b in range(BLOCKS):
-                    nc.scalar.activation(result[:, b, :], scaled[:, b, :], ACT.Relu)
-                    nc.sync.dma_start(out=out_view[:, b, tok], in_=result[:, b, :])
-            elif i < PIECES - 1:
-                nc.scalar.activation(result[:], scaled[:], ACT.Relu)
-                queue = nc.scalar if i == PIECES - 2 else nc.sync
-                queue.dma_start(out=out_view[:, :, tok], in_=result[:])
-            else:
-                for b in range(BLOCKS):
-                    nc.vector.tensor_scalar(result[:, b, :], scaled[:, b, :], 0.0, None, ALU.max)
-                nc.sync.dma_start(out=out_view[:, :, tok], in_=result[:])
+                result = aligned([P, 2, PIECE], F32, name="result%d_%d" % (pair, b))
+                for n in range(2):
+                    i = 2 * pair + n
+                    tok = slice(i * PIECE, (i + 1) * PIECE)
+                    nc.vector.scalar_tensor_tensor(
+                        scaled[:, n, :], acc[i, b][:], c_col[:, b : b + 1], t_picked[:, tok], ALU.mult, ALU.mult
+                    )
+                for n in range(2):
+                    if last:
+                        nc.vector.tensor_scalar(result[:, n, :], scaled[:, n, :], 0.0, None, ALU.max)
+                    else:
+                        nc.scalar.activation(result[:, n, :], scaled[:, n, :], ACT.Relu)
+                queue = nc.scalar if pair == 1 and b == 0 else nc.sync
+                queue.dma_start(
+                    out=out_view[:, b, 2 * pair * PIECE : 2 * (pair + 1) * PIECE],
+                    in_=result[:].rearrange("p n s -> p (n s)"),
+                )

@@ -179,26 +179,35 @@ def tile_picked_tokscale_relu_l_kernel(
             nc.vector.quantize_mx(out=codes1[:].bitcast(FP8X4), scales=scales1[:], in_=woven[i][:].bitcast(BF16))
             for b in range(BLOCKS):
                 product(i, b, 1, codes1[:], scales1[:])
-        for pair in range(2):
-            for b in range(BLOCKS):
-                last = pair == 1 and b == BLOCKS - 1
-                scaled = aligned(
-                    [P, 2, PIECE], F32, name="scaled%d_%d" % (pair, b), tag="stage%d" % ((2 * pair + b + 2) % PIECES)
+        stores = (((0,), (0,)), ((0,), (1,)), ((1,), (0, 1)), ((2, 3), (0,)), ((2, 3), (1,)))
+        scaled = [
+            aligned([P, 2, PIECE], F32, name="scaled%d" % n, tag="stage%d" % ((n + 2) % PIECES)) for n in range(PIECES)
+        ]
+        done = 0
+        for n, (pieces, blocks) in enumerate(stores):
+            last = n == len(stores) - 1
+            result = aligned([P, len(blocks), len(pieces), PIECE], F32, name="result%d" % n)
+            units = [(nb, ni) for ni in range(len(pieces)) for nb in range(len(blocks))]
+            for m, (nb, ni) in enumerate(units):
+                i, b = pieces[ni], blocks[nb]
+                tok = slice(i * PIECE, (i + 1) * PIECE)
+                nc.vector.scalar_tensor_tensor(
+                    scaled[(done + m) // 2][:, (done + m) % 2, :],
+                    acc[i, b][:],
+                    c_col[:, b : b + 1],
+                    t_picked[:, tok],
+                    ALU.mult,
+                    ALU.mult,
                 )
-                result = aligned([P, 2, PIECE], F32, name="result%d_%d" % (pair, b))
-                for n in range(2):
-                    i = 2 * pair + n
-                    tok = slice(i * PIECE, (i + 1) * PIECE)
-                    nc.vector.scalar_tensor_tensor(
-                        scaled[:, n, :], acc[i, b][:], c_col[:, b : b + 1], t_picked[:, tok], ALU.mult, ALU.mult
-                    )
-                for n in range(2):
-                    if last:
-                        nc.vector.tensor_scalar(result[:, n, :], scaled[:, n, :], 0.0, None, ALU.max)
-                    else:
-                        nc.scalar.activation(result[:, n, :], scaled[:, n, :], ACT.Relu)
-                queue = nc.scalar if pair == 1 and b == 0 else nc.sync
-                queue.dma_start(
-                    out=out_view[:, b, 2 * pair * PIECE : 2 * (pair + 1) * PIECE],
-                    in_=result[:].rearrange("p n s -> p (n s)"),
-                )
+            for m, (nb, ni) in enumerate(units):
+                source = scaled[(done + m) // 2][:, (done + m) % 2, :]
+                if last:
+                    nc.vector.tensor_scalar(result[:, nb, ni, :], source, 0.0, None, ALU.max)
+                else:
+                    nc.scalar.activation(result[:, nb, ni, :], source, ACT.Relu)
+            done += len(units)
+            queue = nc.scalar if n == len(stores) - 2 else nc.sync
+            queue.dma_start(
+                out=out_view[:, blocks[0] : blocks[-1] + 1, pieces[0] * PIECE : (pieces[-1] + 1) * PIECE],
+                in_=result[:].rearrange("p b n s -> p b (n s)"),
+            )

@@ -24,7 +24,7 @@ HALF = T // 2
 PIECE = 128
 PIECES = S // PIECE
 CHUNKS = {0: (512, 512), 1: (512, 512), 2: (512, 512), 3: (512, 256, 256)}
-SCALAR_COLS = {(0, 0): 0, (0, 1): 0, (1, 1): 320, (3, 0): 320, (3, 1): 128, (3, 2): 144}
+SCALAR_COLS = {(0, 0): 0, (0, 1): 0, (1, 0): 256, (1, 1): 256, (3, 0): 320, (3, 1): 128, (3, 2): 144}
 OVERLAP_START = T
 
 

@@ -19,13 +19,10 @@ ACT = mybir.ActivationFunctionType
 ALU = mybir.AluOpType
 
 PASSES = 2
+PACK = 4
 BLOCKS = N // P
-HALF = T // 2
 PIECE = 128
 PIECES = S // PIECE
-CHUNKS = {0: (512, 512), 1: (512, 512), 2: (512, 512), 3: (512, 256, 256)}
-SCALAR_COLS = {(0, 0): 0, (0, 1): 0, (1, 0): 256, (1, 1): 256, (3, 0): 320, (3, 1): 128, (3, 2): 144}
-OVERLAP_START = T
 
 
 def tile_picked_tokscale_relu_l_kernel(
@@ -41,28 +38,24 @@ def tile_picked_tokscale_relu_l_kernel(
         def aligned(shape, dtype, name, tag=None):
             return keep.tile(shape, dtype, name=name, tag=tag or name, align_bytes=256)
 
-        x_rows = xT.rearrange("(g p u e) t -> g u p e t", g=PASSES, p=P, u=2, e=2)
-        raw = {}
-
-        def load_x(j, h):
-            first = sum(CHUNKS[j][:h])
-            raw[j, h] = aligned([P, 2, CHUNKS[j][h]], F32, name="raw%d_%d" % (j, h))
-            nc.sync.dma_start(out=raw[j, h][:], in_=x_rows[j // 2, j % 2][:, :, first : first + CHUNKS[j][h]])
-
-        t_small = aligned([P, T // P], F32, name="t_small", tag="pairs1")
-        nc.scalar.dma_start(out=t_small[:], in_=tscale[0:1, :].rearrange("o (p m) -> (o p) m", p=P))
+        x_planes = xT.rearrange("(g p t) c -> g t p c", g=PASSES, p=P, t=PACK)
+        shared = aligned([P, T + S], F32, name="shared")
+        picked = [shared[:, T - S // 2 :].bitcast(BF16).rearrange("p (t s) -> p t s", s=S)]
+        t_window = shared[:, :T]
+        t_small = shared[:, T + 3 * S // 4 - T // P // 2 : T + 3 * S // 4 + T // P // 2]
+        nc.sync.dma_start(out=t_small, in_=tscale[0:1, :].rearrange("o (p m) -> (o p) m", p=P))
         c_col = aligned([P, BLOCKS], F32, name="c_col")
-
         w_words = aligned([P, PASSES, 2 * N], U8, name="w_words")
         w_scales = aligned([P, PASSES, N], U8, name="w_scales")
         nc.gpsimd.memset(w_scales[:].bitcast(I32), 0)
-        for j in range(4):
-            load_x(j, 0)
-            if j == 0:
-                nc.sync.dma_start(offsets[:], offs)
-            for h in range(1, len(CHUNKS[j])):
-                load_x(j, h)
-            if j == 1:
+        raw = {}
+        for g in range(PASSES):
+            for t in range(PACK):
+                raw[g, t] = aligned([P, T], F32, name="raw%d_%d" % (g, t))
+                nc.sync.dma_start(out=raw[g, t][:], in_=x_planes[g, t])
+                if (g, t) == (0, 0):
+                    nc.sync.dma_start(offsets[:], offs)
+            if g == 0:
                 for q in range(4):
                     nc.sync.dma_start(
                         out=w_scales[32 * q : 32 * q + 4].bitcast(I32),
@@ -72,142 +65,112 @@ def tile_picked_tokscale_relu_l_kernel(
         with nc.allow_non_contiguous_dma(reason="one channel scale a partition"):
             nc.sync.dma_start(out=c_col[:], in_=cscale.rearrange("(b p) o -> p (b o)", p=P))
 
-        ident = aligned([P, P], F32, name="ident", tag="pairs2")
+        ident = aligned([P, P], F32, name="ident")
         make_identity(nc, ident[:])
 
-        t_window = aligned([P, T], F32, name="t_window")
-        t_view = t_window[:].rearrange("p (n h m) -> p h n m", h=2, m=4)
+        t_view = t_window.rearrange("p (n h m) -> p h n m", h=2, m=4)
         for h in range(2):
-            bank = psum.tile([P, 4, P], F32, name="t_bank%d" % h, tag="bank%d" % (6 + h))
+            bank = psum.tile([P, 4, P], F32, name="t_bank%d" % h, tag="bank%d" % (4 + h))
             for m in range(4):
                 nc.tensor.transpose(bank[:, m, :], t_small[:, 4 * h + m : 4 * h + m + 1].to_broadcast([P, P]), ident[:])
             nc.scalar.activation(t_view[:, h], bank[:].rearrange("p m n -> p n m"), ACT.Copy)
         t_picked = aligned([P, S], F32, name="t_picked")
-        nc.vector.tensor_copy(t_picked[:], t_window[:].indirect(offsets[:]))
+        nc.vector.tensor_copy(t_picked[:], t_window.indirect(offsets[:]))
 
-        def cast(engine, pairs, j, h, c0, c1):
-            first = sum(CHUNKS[j][:h])
-            dst = pairs[:, 2 * (first + c0) : 2 * (first + c1)].rearrange("p (t e) -> p t e", e=2)
-            src = raw[j, h][:, :, c0:c1].rearrange("p e t -> p t e")
+        slot = {(0, 0): 1, (0, 1): 2, (0, 2): 0, (0, 3): 2, (1, 0): 0, (1, 1): 1, (1, 2): 2, (1, 3): 3}
+        grouped = {}
+
+        def entries(a, b):
+            return offsets[:, a // 16 : b // 16]
+
+        def gather(engine, g, t, a, b):
+            window = raw[g, t][:].indirect(entries(a, b))
             if engine == "scalar":
-                nc.scalar.activation(dst, src, ACT.Copy)
-            elif engine == "vector":
+                nc.scalar.activation(picked[g][:, slot[g, t], a:b], window, ACT.Copy)
+            else:
+                nc.vector.tensor_copy(picked[g][:, slot[g, t], a:b], window)
+
+        def gather_in_place(g, t, a, b):
+            nc.vector.tensor_copy(grouped[g][:, a:b, t], raw[g, t][:].indirect(entries(a, b)))
+
+        def place(g, t0, step, a, b, engine="vector"):
+            first, second = slot[g, t0], slot[g, t0 + step]
+            dst = grouped[g][:, a:b, t0 : t0 + step + 1 : step]
+            src = picked[g][:, first : second + 1 : second - first, a:b].rearrange("p t s -> p s t")
+            if engine == "vector":
                 nc.vector.tensor_copy(dst, src)
             else:
                 nc.gpsimd.tensor_scalar(dst, src, 1.0, 0.0, ALU.mult, ALU.add)
 
-        def make_pairs(j, pairs):
-            for h, width in enumerate(CHUNKS[j]):
-                split = SCALAR_COLS.get((j, h), width)
-                if split > 0:
-                    cast("scalar", pairs, j, h, 0, split)
-                if split < width:
-                    cast("vector" if j == 0 else "gpsimd", pairs, j, h, split, width)
-            return pairs.bitcast(U32)
+        codes = [aligned([P, S], U32, name="codes%d" % g) for g in range(PASSES)]
+        scales = [aligned([P, S], U8, name="scales%d" % g) for g in range(PASSES)]
 
-        half = S // 2
-        picked0 = aligned([P, 2 * S], U32, name="picked0")
-        pairs = aligned([P, 2 * T], BF16, name="pairs0", tag="pairs0")
-        window = make_pairs(0, pairs[:])
-        nc.vector.tensor_copy(
-            picked0[:].rearrange("p (i u s) -> p i u s", u=2, s=half)[:, :, 0, :], window.indirect(offsets[:])
-        )
-        pairs = aligned([P, 2 * T], BF16, name="pairs1", tag="pairs1")
-        window = make_pairs(1, pairs[:])
-        codes0 = aligned([P, S], U32, name="codes0")
-        scales0 = aligned([P, S], U8, name="scales0")
-        woven0 = aligned([P, 2 * S], I32, name="woven0")
-        for i in range(2):
-            nc.vector.tensor_copy(
-                picked0[:, (2 * i + 1) * half : (2 * i + 2) * half],
-                window.indirect(offsets[:, i * half // 16 : (i + 1) * half // 16]),
-            )
-        for i in range(2):
-            nc.vector.tensor_copy(
-                woven0[:, i * S : (i + 1) * S].rearrange("p (s u) -> p s u", u=2),
-                picked0[:, i * S : (i + 1) * S].bitcast(I32).rearrange("p (u s) -> p s u", u=2),
-            )
-        for i in range(2):
+        def quantise(g, a, b):
             nc.vector.quantize_mx(
-                out=codes0[:, i * half : (i + 1) * half].bitcast(FP8X4),
-                scales=scales0[:, i * half : (i + 1) * half],
-                in_=woven0[:, i * S : (i + 1) * S].bitcast(BF16),
+                out=codes[g][:, a:b].bitcast(FP8X4),
+                scales=scales[g][:, a:b],
+                in_=grouped[g][:, a:b, :].rearrange("p s t -> p (s t)"),
             )
 
-        acc = {}
+        acc = [psum.tile([P, BLOCKS, PIECE], F32, name="acc%d" % i, tag="bank%d" % i) for i in range(PIECES)]
 
-        def product(i, b, g, codes, scales):
-            nc.tensor.matmul_mx(
-                out=acc[i, b][:],
-                lhsT=w_words[:, g, 2 * P * b : 2 * P * (b + 1)].bitcast(FP4X4),
-                lhsT_scale=w_scales[:, g, P * b : P * (b + 1)],
-                rhs=codes.bitcast(FP8X4),
-                rhs_scale=scales,
-                start=(g == 0),
-                stop=(g == PASSES - 1),
-            )
-
-        for i in range(PIECES):
+        def products(g, i):
             tok = slice(i * PIECE, (i + 1) * PIECE)
             for b in range(BLOCKS):
-                acc[i, b] = psum.tile([P, PIECE], F32, name="acc%d_%d" % (i, b), tag="bank%d" % (2 * i + b))
-                product(i, b, 0, codes0[:, tok], scales0[:, tok])
-
-        picked1 = aligned([P, 2 * S], U32, name="picked1")
-        pairs = aligned([P, 2 * (OVERLAP_START + T)], BF16, name="pairs2", tag="pairs2")
-        window = make_pairs(2, pairs[:, 2 * OVERLAP_START :])
-        nc.vector.tensor_copy(
-            picked1[:].rearrange("p (i u s) -> p i u s", u=2, s=PIECE)[:, :, 0, :], window.indirect(offsets[:])
-        )
-        window = make_pairs(3, pairs[:, : 2 * T])
-        out_view = out.rearrange("(b p) s -> p b s", p=P)
-        cols = PIECE // 16
-        woven = {}
-        for i in range(PIECES):
-            nc.vector.tensor_copy(
-                picked1[:, (2 * i + 1) * PIECE : (2 * i + 2) * PIECE],
-                window.indirect(offsets[:, i * cols : (i + 1) * cols]),
-            )
-            woven[i] = aligned([P, 2 * PIECE], U32, name="woven1_%d" % i, tag="stage%d" % i)
-            nc.scalar.copy(
-                woven[i][:].rearrange("p (s u) -> p s u", u=2),
-                picked1[:, 2 * i * PIECE : (2 * i + 2) * PIECE].rearrange("p (u s) -> p s u", u=2),
-            )
-        for i in range(PIECES):
-            codes1 = aligned([P, PIECE], U32, name="codes1_%d" % i)
-            scales1 = aligned([P, PIECE], U8, name="scales1_%d" % i)
-            nc.vector.quantize_mx(out=codes1[:].bitcast(FP8X4), scales=scales1[:], in_=woven[i][:].bitcast(BF16))
-            for b in range(BLOCKS):
-                product(i, b, 1, codes1[:], scales1[:])
-        stores = (((0,), (0,)), ((0,), (1,)), ((1,), (0, 1)), ((2, 3), (0,)), ((2, 3), (1,)))
-        scaled = [
-            aligned([P, 2, PIECE], F32, name="scaled%d" % n, tag="stage%d" % ((n + 2) % PIECES)) for n in range(PIECES)
-        ]
-        done = 0
-        for n, (pieces, blocks) in enumerate(stores):
-            last = n == len(stores) - 1
-            result = aligned([P, len(blocks), len(pieces), PIECE], F32, name="result%d" % n)
-            units = [(nb, ni) for ni in range(len(pieces)) for nb in range(len(blocks))]
-            for m, (nb, ni) in enumerate(units):
-                i, b = pieces[ni], blocks[nb]
-                tok = slice(i * PIECE, (i + 1) * PIECE)
-                nc.vector.scalar_tensor_tensor(
-                    scaled[(done + m) // 2][:, (done + m) % 2, :],
-                    acc[i, b][:],
-                    c_col[:, b : b + 1],
-                    t_picked[:, tok],
-                    ALU.mult,
-                    ALU.mult,
+                nc.tensor.matmul_mx(
+                    out=acc[i][:, b, :],
+                    lhsT=w_words[:, g, 2 * P * b : 2 * P * (b + 1)].bitcast(FP4X4),
+                    lhsT_scale=w_scales[:, g, P * b : P * (b + 1)],
+                    rhs=codes[g][:, tok].bitcast(FP8X4),
+                    rhs_scale=scales[g][:, tok],
+                    start=(g == 0 and b == 0),
+                    stop=(g == PASSES - 1 and b == BLOCKS - 1),
                 )
-            for m, (nb, ni) in enumerate(units):
-                source = scaled[(done + m) // 2][:, (done + m) % 2, :]
-                if last:
-                    nc.vector.tensor_scalar(result[:, nb, ni, :], source, 0.0, None, ALU.max)
-                else:
-                    nc.scalar.activation(result[:, nb, ni, :], source, ACT.Relu)
-            done += len(units)
-            queue = nc.scalar if n == len(stores) - 2 else nc.sync
-            queue.dma_start(
-                out=out_view[:, blocks[0] : blocks[-1] + 1, pieces[0] * PIECE : (pieces[-1] + 1) * PIECE],
-                in_=result[:].rearrange("p b n s -> p b (n s)"),
+
+        half = S // 2
+        grouped[0] = aligned([P, S, PACK], BF16, name="grouped0", tag="grouped")
+        gather("vector", 0, 0, 0, S)
+        for a in (0, half):
+            gather("scalar", 0, 1, a, a + half)
+            place(0, 0, 1, a, a + half, "gpsimd")
+        gather("vector", 0, 2, 0, S)
+        for a in (0, half):
+            gather("scalar", 0, 3, a, a + half)
+        place(0, 2, 1, 0, half)
+        place(0, 2, 1, half, S)
+        quantise(0, 0, half)
+        quantise(0, half, S)
+        for i in range(PIECES):
+            products(0, i)
+
+        grouped[1] = aligned([P, S, PACK], BF16, name="grouped1", tag="grouped")
+        picked1 = aligned([P, PACK, S], BF16, name="picked1", tag="raw0_3")
+        picked.append(picked1[:])
+        gather("scalar", 1, 0, PIECE, S)
+        gather("scalar", 1, 1, PIECE, S)
+        gather_in_place(1, 0, 0, PIECE)
+        gather_in_place(1, 1, 0, PIECE)
+        gather_in_place(1, 2, 0, PIECE)
+        place(1, 0, 1, PIECE, S)
+        gather("scalar", 1, 2, PIECE, S)
+        gather_in_place(1, 3, 0, PIECE)
+        for i in range(1, PIECES):
+            gather("scalar", 1, 3, i * PIECE, (i + 1) * PIECE)
+        place(1, 2, 1, PIECE, 2 * PIECE)
+        for i in range(PIECES):
+            quantise(1, i * PIECE, (i + 1) * PIECE)
+            products(1, i)
+            if i + 2 < PIECES:
+                place(1, 2, 1, (i + 2) * PIECE, (i + 3) * PIECE)
+
+        out_view = out.rearrange("(b p) s -> p b s", p=P)
+        for i in range(PIECES):
+            tok = slice(i * PIECE, (i + 1) * PIECE)
+            scaled = aligned([P, BLOCKS, PIECE], F32, name="scaled%d" % i)
+            nc.vector.tensor_tensor(
+                scaled[:], acc[i][:], t_picked[:, tok].unsqueeze(1).to_broadcast([P, BLOCKS, PIECE]), ALU.mult
             )
+            result = aligned([P, BLOCKS, PIECE], F32, name="result%d" % i)
+            for b in range(BLOCKS):
+                nc.scalar.activation(result[:, b, :], scaled[:, b, :], ACT.Relu, scale=c_col[:, b : b + 1])
+            nc.sync.dma_start(out=out_view[:, :, tok], in_=result[:])

@@ -39,13 +39,13 @@ def tile_picked_tokscale_relu_l_kernel(
             return keep.tile(shape, dtype, name=name, tag=tag or name, align_bytes=256)
 
         x_planes = xT.rearrange("(g p t) c -> g t p c", g=PASSES, p=P, t=PACK)
-        shared = aligned([P, T + S], F32, name="shared")
-        picked = [shared[:, T - S // 2 :].bitcast(BF16).rearrange("p (t s) -> p t s", s=S)]
-        t_window = shared[:, :T]
-        t_small = shared[:, T + 3 * S // 4 - T // P // 2 : T + 3 * S // 4 + T // P // 2]
+        shared = aligned([P, 3 * S // 2], F32, name="shared")
+        picked = [shared[:].bitcast(BF16).rearrange("p (t s) -> p t s", s=S)]
+        t_window = aligned([P, T], F32, name="t_window")
+        t_small = shared[:, 3 * S // 2 - T // P :]
         nc.sync.dma_start(out=t_small, in_=tscale[0:1, :].rearrange("o (p m) -> (o p) m", p=P))
         c_col = aligned([P, BLOCKS], F32, name="c_col")
-        w_words = aligned([P, PASSES, 2 * N], U8, name="w_words")
+        w_words = [aligned([P, 2 * N], U8, name="w_words%d" % g) for g in range(PASSES)]
         w_scales = aligned([P, PASSES, N], U8, name="w_scales")
         nc.gpsimd.memset(w_scales[:].bitcast(I32), 0)
         raw = {}
@@ -61,21 +61,21 @@ def tile_picked_tokscale_relu_l_kernel(
                         out=w_scales[32 * q : 32 * q + 4].bitcast(I32),
                         in_=w1_scales[:, 4 * q : 4 * q + 4, :].rearrange("z r n -> r z n").bitcast(I32),
                     )
-        nc.sync.dma_start(out=w_words[:].bitcast(I32), in_=w1_words.rearrange("z p n -> p z n").bitcast(I32))
+                nc.sync.dma_start(out=w_words[0][:].bitcast(I32), in_=w1_words[0].bitcast(I32))
+        nc.sync.dma_start(out=w_words[1][:].bitcast(I32), in_=w1_words[1].bitcast(I32))
         with nc.allow_non_contiguous_dma(reason="one channel scale a partition"):
             nc.sync.dma_start(out=c_col[:], in_=cscale.rearrange("(b p) o -> p (b o)", p=P))
 
         ident = aligned([P, P], F32, name="ident")
         make_identity(nc, ident[:])
 
-        t_view = t_window.rearrange("p (n h m) -> p h n m", h=2, m=4)
+        t_view = t_window[:].rearrange("p (n h m) -> p h n m", h=2, m=4)
         for h in range(2):
             bank = psum.tile([P, 4, P], F32, name="t_bank%d" % h, tag="bank%d" % (4 + h))
             for m in range(4):
                 nc.tensor.transpose(bank[:, m, :], t_small[:, 4 * h + m : 4 * h + m + 1].to_broadcast([P, P]), ident[:])
             nc.scalar.activation(t_view[:, h], bank[:].rearrange("p m n -> p n m"), ACT.Copy)
         t_picked = aligned([P, S], F32, name="t_picked")
-        nc.vector.tensor_copy(t_picked[:], t_window.indirect(offsets[:]))
 
         slot = {(0, 0): 1, (0, 1): 2, (0, 2): 0, (0, 3): 2, (1, 0): 0, (1, 1): 1, (1, 2): 2, (1, 3): 3}
         grouped = {}
@@ -112,30 +112,35 @@ def tile_picked_tokscale_relu_l_kernel(
                 in_=grouped[g][:, a:b, :].rearrange("p s t -> p (s t)"),
             )
 
-        acc = [psum.tile([P, BLOCKS, PIECE], F32, name="acc%d" % i, tag="bank%d" % i) for i in range(PIECES)]
+        last = PIECES - 1
+        acc = {}
+        for i in range(last):
+            acc[i] = psum.tile([P, BLOCKS, PIECE], F32, name="acc%d" % i, tag="bank%d" % i)
+        last_acc = [psum.tile([P, PIECE], F32, name="last%d" % b, tag="bank%d" % (6 + b)) for b in range(BLOCKS)]
 
         def products(g, i):
             tok = slice(i * PIECE, (i + 1) * PIECE)
             for b in range(BLOCKS):
                 nc.tensor.matmul_mx(
-                    out=acc[i][:, b, :],
-                    lhsT=w_words[:, g, 2 * P * b : 2 * P * (b + 1)].bitcast(FP4X4),
+                    out=last_acc[b][:] if i == last else acc[i][:, b, :],
+                    lhsT=w_words[g][:, 2 * P * b : 2 * P * (b + 1)].bitcast(FP4X4),
                     lhsT_scale=w_scales[:, g, P * b : P * (b + 1)],
                     rhs=codes[g][:, tok].bitcast(FP8X4),
                     rhs_scale=scales[g][:, tok],
-                    start=(g == 0 and b == 0),
-                    stop=(g == PASSES - 1 and b == BLOCKS - 1),
+                    start=(g == 0 and (b == 0 or i == last)),
+                    stop=(g == PASSES - 1 and (b == BLOCKS - 1 or i == last)),
                 )
 
         half = S // 2
         grouped[0] = aligned([P, S, PACK], BF16, name="grouped0", tag="grouped")
         gather("vector", 0, 0, 0, S)
-        for a in (0, half):
-            gather("scalar", 0, 1, a, a + half)
+        for a, engine in ((0, "vector"), (half, "scalar")):
+            gather(engine, 0, 1, a, a + half)
             place(0, 0, 1, a, a + half, "gpsimd")
+        nc.scalar.activation(t_picked[:], t_window[:].indirect(offsets[:]), ACT.Copy)
         gather("vector", 0, 2, 0, S)
-        for a in (0, half):
-            gather("scalar", 0, 3, a, a + half)
+        for a, engine in ((0, "vector"), (half, "scalar")):
+            gather(engine, 0, 3, a, a + half)
         place(0, 2, 1, 0, half)
         place(0, 2, 1, half, S)
         quantise(0, 0, half)
@@ -150,8 +155,8 @@ def tile_picked_tokscale_relu_l_kernel(
         gather("scalar", 1, 1, PIECE, S)
         gather_in_place(1, 0, 0, PIECE)
         gather_in_place(1, 1, 0, PIECE)
-        gather_in_place(1, 2, 0, PIECE)
         place(1, 0, 1, PIECE, S)
+        gather_in_place(1, 2, 0, PIECE)
         gather("scalar", 1, 2, PIECE, S)
         gather_in_place(1, 3, 0, PIECE)
         for i in range(1, PIECES):
@@ -164,7 +169,7 @@ def tile_picked_tokscale_relu_l_kernel(
                 place(1, 2, 1, (i + 2) * PIECE, (i + 3) * PIECE)
 
         out_view = out.rearrange("(b p) s -> p b s", p=P)
-        for i in range(PIECES):
+        for i in range(last):
             tok = slice(i * PIECE, (i + 1) * PIECE)
             scaled = aligned([P, BLOCKS, PIECE], F32, name="scaled%d" % i)
             nc.vector.tensor_tensor(
@@ -174,3 +179,11 @@ def tile_picked_tokscale_relu_l_kernel(
             for b in range(BLOCKS):
                 nc.scalar.activation(result[:, b, :], scaled[:, b, :], ACT.Relu, scale=c_col[:, b : b + 1])
             nc.sync.dma_start(out=out_view[:, :, tok], in_=result[:])
+        tok = slice(last * PIECE, S)
+        for b in range(BLOCKS):
+            scaled = aligned([P, PIECE], F32, name="last_scaled%d" % b)
+            nc.vector.tensor_tensor(scaled[:], last_acc[b][:], t_picked[:, tok], ALU.mult)
+            result = aligned([P, PIECE], F32, name="last_result%d" % b)
+            nc.scalar.activation(result[:], scaled[:], ACT.Relu, scale=c_col[:, b : b + 1])
+            queue = nc.sync if b == 0 else nc.scalar
+            queue.dma_start(out=out_view[:, b, tok], in_=result[:])

@@ -61,8 +61,8 @@ def tile_picked_tokscale_relu_l_kernel(
                         out=w_scales[32 * q : 32 * q + 4].bitcast(I32),
                         in_=w1_scales[:, 4 * q : 4 * q + 4, :].rearrange("z r n -> r z n").bitcast(I32),
                     )
-                nc.sync.dma_start(out=w_words[0][:].bitcast(I32), in_=w1_words[0].bitcast(I32))
-        nc.sync.dma_start(out=w_words[1][:].bitcast(I32), in_=w1_words[1].bitcast(I32))
+        for g in range(PASSES):
+            nc.sync.dma_start(out=w_words[g][:].bitcast(I32), in_=w1_words[g].bitcast(I32))
         with nc.allow_non_contiguous_dma(reason="one channel scale a partition"):
             nc.sync.dma_start(out=c_col[:], in_=cscale.rearrange("(b p) o -> p (b o)", p=P))
 

@@ -23,6 +23,7 @@ PACK = 4
 BLOCKS = N // P
 PIECE = 128
 PIECES = S // PIECE
+LOAD_ORDER = ((0, 1, 3, 2), (0, 1, 2, 3))
 
 
 def tile_picked_tokscale_relu_l_kernel(
@@ -39,10 +40,14 @@ def tile_picked_tokscale_relu_l_kernel(
             return keep.tile(shape, dtype, name=name, tag=tag or name, align_bytes=256)
 
         x_planes = xT.rearrange("(g p t) c -> g t p c", g=PASSES, p=P, t=PACK)
-        shared = aligned([P, 3 * S // 2], F32, name="shared")
-        picked = [shared[:].bitcast(BF16).rearrange("p (t s) -> p t s", s=S)]
-        t_window = aligned([P, T], F32, name="t_window")
-        t_small = shared[:, 3 * S // 2 - T // P :]
+        shared = aligned([P, S + T], F32, name="shared")
+        t_window = shared[:, S:]
+        pairs = {
+            (0, 0): shared[:, :S].bitcast(BF16).rearrange("p (t s) -> p t s", t=2),
+            (0, 1): shared[:, 3 * S // 4 : 7 * S // 4].bitcast(BF16).rearrange("p (t s) -> p t s", t=2),
+        }
+        t_tile = aligned([P, T // P], F32, name="t_small")
+        t_small = t_tile[:]
         nc.sync.dma_start(out=t_small, in_=tscale[0:1, :].rearrange("o (p m) -> (o p) m", p=P))
         c_col = aligned([P, BLOCKS], F32, name="c_col")
         w_words = [aligned([P, 2 * N], U8, name="w_words%d" % g) for g in range(PASSES)]
@@ -50,7 +55,7 @@ def tile_picked_tokscale_relu_l_kernel(
         nc.gpsimd.memset(w_scales[:].bitcast(I32), 0)
         raw = {}
         for g in range(PASSES):
-            for t in range(PACK):
+            for t in LOAD_ORDER[g]:
                 raw[g, t] = aligned([P, T], F32, name="raw%d_%d" % (g, t))
                 nc.sync.dma_start(out=raw[g, t][:], in_=x_planes[g, t])
                 if (g, t) == (0, 0):
@@ -69,7 +74,7 @@ def tile_picked_tokscale_relu_l_kernel(
         ident = aligned([P, P], F32, name="ident")
         make_identity(nc, ident[:])
 
-        t_view = t_window[:].rearrange("p (n h m) -> p h n m", h=2, m=4)
+        t_view = t_window.rearrange("p (n h m) -> p h n m", h=2, m=4)
         for h in range(2):
             bank = psum.tile([P, 4, P], F32, name="t_bank%d" % h, tag="bank%d" % (4 + h))
             for m in range(4):
@@ -77,7 +82,6 @@ def tile_picked_tokscale_relu_l_kernel(
             nc.scalar.activation(t_view[:, h], bank[:].rearrange("p m n -> p n m"), ACT.Copy)
         t_picked = aligned([P, S], F32, name="t_picked")
 
-        slot = {(0, 0): 1, (0, 1): 2, (0, 2): 0, (0, 3): 2, (1, 0): 0, (1, 1): 1, (1, 2): 2, (1, 3): 3}
         grouped = {}
 
         def entries(a, b):
@@ -86,21 +90,17 @@ def tile_picked_tokscale_relu_l_kernel(
         def gather(engine, g, t, a, b):
             window = raw[g, t][:].indirect(entries(a, b))
             if engine == "scalar":
-                nc.scalar.activation(picked[g][:, slot[g, t], a:b], window, ACT.Copy)
+                nc.scalar.activation(pairs[g, t // 2][:, t % 2, a:b], window, ACT.Copy)
             else:
-                nc.vector.tensor_copy(picked[g][:, slot[g, t], a:b], window)
+                nc.vector.tensor_copy(pairs[g, t // 2][:, t % 2, a:b], window)
 
         def gather_in_place(g, t, a, b):
             nc.vector.tensor_copy(grouped[g][:, a:b, t], raw[g, t][:].indirect(entries(a, b)))
 
-        def place(g, t0, step, a, b, engine="vector"):
-            first, second = slot[g, t0], slot[g, t0 + step]
-            dst = grouped[g][:, a:b, t0 : t0 + step + 1 : step]
-            src = picked[g][:, first : second + 1 : second - first, a:b].rearrange("p t s -> p s t")
-            if engine == "vector":
-                nc.vector.tensor_copy(dst, src)
-            else:
-                nc.gpsimd.tensor_scalar(dst, src, 1.0, 0.0, ALU.mult, ALU.add)
+        def place(g, u, a, b):
+            nc.vector.tensor_copy(
+                grouped[g][:, a:b, 2 * u : 2 * u + 2], pairs[g, u][:, :, a:b].rearrange("p t s -> p s t")
+            )
 
         codes = [aligned([P, S], U32, name="codes%d" % g) for g in range(PASSES)]
         scales = [aligned([P, S], U8, name="scales%d" % g) for g in range(PASSES)]
@@ -134,39 +134,39 @@ def tile_picked_tokscale_relu_l_kernel(
         half = S // 2
         grouped[0] = aligned([P, S, PACK], BF16, name="grouped0", tag="grouped")
         gather("vector", 0, 0, 0, S)
-        for a, engine in ((0, "vector"), (half, "scalar")):
-            gather(engine, 0, 1, a, a + half)
-            place(0, 0, 1, a, a + half, "gpsimd")
-        nc.scalar.activation(t_picked[:], t_window[:].indirect(offsets[:]), ACT.Copy)
-        gather("vector", 0, 2, 0, S)
-        for a, engine in ((0, "vector"), (half, "scalar")):
-            gather(engine, 0, 3, a, a + half)
-        place(0, 2, 1, 0, half)
-        place(0, 2, 1, half, S)
+        gather("vector", 0, 1, 0, S)
+        nc.scalar.activation(t_picked[:], t_window.indirect(offsets[:]), ACT.Copy)
+        gather("scalar", 0, 3, 0, S)
+        place(0, 0, half, S)
+        place(0, 0, 0, half)
+        gather("vector", 0, 2, 0, half)
+        gather("scalar", 0, 2, half, S)
+        place(0, 1, 0, half)
+        place(0, 1, half, S)
         quantise(0, 0, half)
         quantise(0, half, S)
         for i in range(PIECES):
             products(0, i)
 
         grouped[1] = aligned([P, S, PACK], BF16, name="grouped1", tag="grouped")
-        picked1 = aligned([P, PACK, S], BF16, name="picked1", tag="raw0_3")
-        picked.append(picked1[:])
+        picked1 = aligned([P, PACK, S], BF16, name="picked1", tag="raw0_2")
+        pairs[1, 0] = picked1[:, 0:2, :]
+        pairs[1, 1] = picked1[:, 2:4, :]
         gather("scalar", 1, 0, PIECE, S)
         gather("scalar", 1, 1, PIECE, S)
-        gather_in_place(1, 0, 0, PIECE)
-        gather_in_place(1, 1, 0, PIECE)
-        place(1, 0, 1, PIECE, S)
-        gather_in_place(1, 2, 0, PIECE)
+        for t in range(PACK - 1):
+            gather_in_place(1, t, 0, PIECE)
+        place(1, 0, PIECE, S)
         gather("scalar", 1, 2, PIECE, S)
         gather_in_place(1, 3, 0, PIECE)
         for i in range(1, PIECES):
             gather("scalar", 1, 3, i * PIECE, (i + 1) * PIECE)
-        place(1, 2, 1, PIECE, 2 * PIECE)
+        place(1, 1, PIECE, 2 * PIECE)
         for i in range(PIECES):
             quantise(1, i * PIECE, (i + 1) * PIECE)
             products(1, i)
             if i + 2 < PIECES:
-                place(1, 2, 1, (i + 2) * PIECE, (i + 3) * PIECE)
+                place(1, 1, (i + 2) * PIECE, (i + 3) * PIECE)
 
         out_view = out.rearrange("(b p) s -> p b s", p=P)
         for i in range(last):

@@ -66,7 +66,6 @@ def tile_picked_tokscale_relu_l_kernel(
                         out=w_scales[32 * q : 32 * q + 4].bitcast(I32),
                         in_=w1_scales[:, 4 * q : 4 * q + 4, :].rearrange("z r n -> r z n").bitcast(I32),
                     )
-        for g in range(PASSES):
             nc.sync.dma_start(out=w_words[g][:].bitcast(I32), in_=w1_words[g].bitcast(I32))
         with nc.allow_non_contiguous_dma(reason="one channel scale a partition"):
             nc.sync.dma_start(out=c_col[:], in_=cscale.rearrange("(b p) o -> p (b o)", p=P))
@@ -97,10 +96,8 @@ def tile_picked_tokscale_relu_l_kernel(
         def gather_in_place(g, t, a, b):
             nc.vector.tensor_copy(grouped[g][:, a:b, t], raw[g, t][:].indirect(entries(a, b)))
 
-        def place(g, u, a, b):
-            nc.vector.tensor_copy(
-                grouped[g][:, a:b, 2 * u : 2 * u + 2], pairs[g, u][:, :, a:b].rearrange("p t s -> p s t")
-            )
+        def place(g, u, a, b, copy=nc.vector.tensor_copy):
+            copy(grouped[g][:, a:b, 2 * u : 2 * u + 2], pairs[g, u][:, :, a:b].rearrange("p t s -> p s t"))
 
         codes = [aligned([P, S], U32, name="codes%d" % g) for g in range(PASSES)]
         scales = [aligned([P, S], U8, name="scales%d" % g) for g in range(PASSES)]
@@ -166,7 +163,7 @@ def tile_picked_tokscale_relu_l_kernel(
             quantise(1, i * PIECE, (i + 1) * PIECE)
             products(1, i)
             if i + 2 < PIECES:
-                place(1, 1, (i + 2) * PIECE, (i + 3) * PIECE)
+                place(1, 1, (i + 2) * PIECE, (i + 3) * PIECE, nc.scalar.copy if i == 1 else nc.vector.tensor_copy)
 
         out_view = out.rearrange("(b p) s -> p b s", p=P)
         for i in range(last):
@@ -185,5 +182,4 @@ def tile_picked_tokscale_relu_l_kernel(
             nc.vector.tensor_tensor(scaled[:], last_acc[b][:], t_picked[:, tok], ALU.mult)
             result = aligned([P, PIECE], F32, name="last_result%d" % b)
             nc.scalar.activation(result[:], scaled[:], ACT.Relu, scale=c_col[:, b : b + 1])
-            queue = nc.sync if b == 0 else nc.scalar
-            queue.dma_start(out=out_view[:, b, tok], in_=result[:])
+            nc.sync.dma_start(out=out_view[:, b, tok], in_=result[:])

@@ -60,13 +60,14 @@ def tile_picked_tokscale_relu_l_kernel(
                 nc.sync.dma_start(out=raw[g, t][:], in_=x_planes[g, t])
                 if (g, t) == (0, 0):
                     nc.sync.dma_start(offsets[:], offs)
-            if g == 0:
-                for q in range(4):
-                    nc.sync.dma_start(
-                        out=w_scales[32 * q : 32 * q + 4].bitcast(I32),
-                        in_=w1_scales[:, 4 * q : 4 * q + 4, :].rearrange("z r n -> r z n").bitcast(I32),
-                    )
-            nc.sync.dma_start(out=w_words[g][:].bitcast(I32), in_=w1_words[g].bitcast(I32))
+                if (g, t) == (1, 2):
+                    nc.sync.dma_start(out=w_words[0][:].bitcast(I32), in_=w1_words[0].bitcast(I32))
+                    for q in range(4):
+                        nc.sync.dma_start(
+                            out=w_scales[32 * q : 32 * q + 4].bitcast(I32),
+                            in_=w1_scales[:, 4 * q : 4 * q + 4, :].rearrange("z r n -> r z n").bitcast(I32),
+                        )
+        nc.sync.dma_start(out=w_words[1][:].bitcast(I32), in_=w1_words[1].bitcast(I32))
         with nc.allow_non_contiguous_dma(reason="one channel scale a partition"):
             nc.sync.dma_start(out=c_col[:], in_=cscale.rearrange("(b p) o -> p (b o)", p=P))
 

@@ -42,10 +42,8 @@ def tile_picked_tokscale_relu_l_kernel(
         x_planes = xT.rearrange("(g p t) c -> g t p c", g=PASSES, p=P, t=PACK)
         shared = aligned([P, S + T], F32, name="shared")
         t_window = shared[:, S:]
-        pairs = {
-            (0, 0): shared[:, :S].bitcast(BF16).rearrange("p (t s) -> p t s", t=2),
-            (0, 1): shared[:, 3 * S // 4 : 7 * S // 4].bitcast(BF16).rearrange("p (t s) -> p t s", t=2),
-        }
+        picked0 = shared[:, : 2 * S].bitcast(BF16).rearrange("p (t s) -> p t s", t=PACK)
+        pairs = {(0, 0): picked0[:, 0:2, :], (0, 1): picked0[:, 2:4, :]}
         t_tile = aligned([P, T // P], F32, name="t_small")
         t_small = t_tile[:]
         nc.sync.dma_start(out=t_small, in_=tscale[0:1, :].rearrange("o (p m) -> (o p) m", p=P))
@@ -61,13 +59,13 @@ def tile_picked_tokscale_relu_l_kernel(
                 if (g, t) == (0, 0):
                     nc.sync.dma_start(offsets[:], offs)
                 if (g, t) == (1, 2):
-                    nc.sync.dma_start(out=w_words[0][:].bitcast(I32), in_=w1_words[0].bitcast(I32))
                     for q in range(4):
                         nc.sync.dma_start(
                             out=w_scales[32 * q : 32 * q + 4].bitcast(I32),
                             in_=w1_scales[:, 4 * q : 4 * q + 4, :].rearrange("z r n -> r z n").bitcast(I32),
                         )
-        nc.sync.dma_start(out=w_words[1][:].bitcast(I32), in_=w1_words[1].bitcast(I32))
+        for g in range(PASSES):
+            nc.sync.dma_start(out=w_words[g][:].bitcast(I32), in_=w1_words[g].bitcast(I32))
         with nc.allow_non_contiguous_dma(reason="one channel scale a partition"):
             nc.sync.dma_start(out=c_col[:], in_=cscale.rearrange("(b p) o -> p (b o)", p=P))
 
@@ -134,13 +132,14 @@ def tile_picked_tokscale_relu_l_kernel(
         gather("vector", 0, 0, 0, S)
         gather("vector", 0, 1, 0, S)
         nc.scalar.activation(t_picked[:], t_window.indirect(offsets[:]), ACT.Copy)
-        gather("scalar", 0, 3, 0, S)
-        place(0, 0, half, S)
-        place(0, 0, 0, half)
-        gather("vector", 0, 2, 0, half)
-        gather("scalar", 0, 2, half, S)
-        place(0, 1, 0, half)
-        place(0, 1, half, S)
+        for t in (3, 2):
+            gather("vector", 0, t, 0, half)
+            gather("scalar", 0, t, half, S)
+        for a in (0, half):
+            nc.vector.tensor_copy(
+                grouped[0][:, a : a + half, :].rearrange("p (c i) t -> p c t i", i=4),
+                picked0[:, :, a : a + half].rearrange("p t (c i) -> p c t i", i=4),
+            )
         quantise(0, 0, half)
         quantise(0, half, S)
         for i in range(PIECES):

@@ -58,7 +58,7 @@ def tile_picked_tokscale_relu_l_kernel(
                 nc.sync.dma_start(out=raw[g, t][:], in_=x_planes[g, t])
                 if (g, t) == (0, 0):
                     nc.sync.dma_start(offsets[:], offs)
-                if (g, t) == (1, 2):
+                if (g, t) == (0, 3):
                     for q in range(4):
                         nc.sync.dma_start(
                             out=w_scales[32 * q : 32 * q + 4].bitcast(I32),

from contextlib import ExitStack

import concourse.mybir as mybir
from concourse.masks import make_identity

K, T, S, N = 1024, 1024, 512, 256
P = 128
FLOPS = 2 * K * S * N

F32 = mybir.dt.float32
BF16 = mybir.dt.bfloat16
I32 = mybir.dt.int32
U32 = mybir.dt.uint32
U16 = mybir.dt.uint16
U8 = mybir.dt.uint8
FP8X4 = mybir.dt.float8_e4m3fn_x4
FP4X4 = mybir.dt.float4_e2m1fn_x4
ACT = mybir.ActivationFunctionType
ALU = mybir.AluOpType

PASSES = 2
PACK = 4
BLOCKS = N // P
PIECE = 128
PIECES = S // PIECE
LOAD_ORDER = ((0, 1, 3, 2), (0, 1, 2, 3))


def tile_picked_tokscale_relu_l_kernel(
    tc, xT, tscale, cscale, w1_words, w1_scales, offs, out
):
    nc = tc.nc
    with ExitStack() as ctx:
        keep = ctx.enter_context(tc.tile_pool(name="keep", bufs=1))
        psum = ctx.enter_context(tc.psum_pool(name="psum", bufs=1))

        offsets = keep.tile([P, S // 16], U16, name="offsets")

        def aligned(shape, dtype, name, tag=None):
            return keep.tile(shape, dtype, name=name, tag=tag or name, align_bytes=256)

        x_planes = xT.rearrange("(g p t) c -> g t p c", g=PASSES, p=P, t=PACK)
        shared = aligned([P, S + T], F32, name="shared")
        t_window = shared[:, S:]
        picked0 = shared[:, : 2 * S].bitcast(BF16).rearrange("p (t s) -> p t s", t=PACK)
        pairs = {(0, 0): picked0[:, 0:2, :], (0, 1): picked0[:, 2:4, :]}
        t_tile = aligned([P, T // P], F32, name="t_small")
        t_small = t_tile[:]
        nc.sync.dma_start(out=t_small, in_=tscale[0:1, :].rearrange("o (p m) -> (o p) m", p=P))
        c_col = aligned([P, BLOCKS], F32, name="c_col")
        w_words = [aligned([P, 2 * N], U8, name="w_words%d" % g) for g in range(PASSES)]
        w_scales = aligned([P, PASSES, N], U8, name="w_scales")
        nc.gpsimd.memset(w_scales[:].bitcast(I32), 0)
        raw = {}
        for g in range(PASSES):
            for t in LOAD_ORDER[g]:
                raw[g, t] = aligned([P, T], F32, name="raw%d_%d" % (g, t))
                nc.sync.dma_start(out=raw[g, t][:], in_=x_planes[g, t])
                if (g, t) == (0, 0):
                    nc.sync.dma_start(offsets[:], offs)
                if (g, t) == (0, 3):
                    for q in range(4):
                        nc.sync.dma_start(
                            out=w_scales[32 * q : 32 * q + 4].bitcast(I32),
                            in_=w1_scales[:, 4 * q : 4 * q + 4, :].rearrange("z r n -> r z n").bitcast(I32),
                        )
        for g in range(PASSES):
            nc.sync.dma_start(out=w_words[g][:].bitcast(I32), in_=w1_words[g].bitcast(I32))
        with nc.allow_non_contiguous_dma(reason="one channel scale a partition"):
            nc.sync.dma_start(out=c_col[:], in_=cscale.rearrange("(b p) o -> p (b o)", p=P))

        ident = aligned([P, P], F32, name="ident")
        make_identity(nc, ident[:])

        t_view = t_window.rearrange("p (n h m) -> p h n m", h=2, m=4)
        for h in range(2):
            bank = psum.tile([P, 4, P], F32, name="t_bank%d" % h, tag="bank%d" % (4 + h))
            for m in range(4):
                nc.tensor.transpose(bank[:, m, :], t_small[:, 4 * h + m : 4 * h + m + 1].to_broadcast([P, P]), ident[:])
            nc.scalar.activation(t_view[:, h], bank[:].rearrange("p m n -> p n m"), ACT.Copy)
        t_picked = aligned([P, S], F32, name="t_picked")

        grouped = {}

        def entries(a, b):
            return offsets[:, a // 16 : b // 16]

        def gather(engine, g, t, a, b):
            window = raw[g, t][:].indirect(entries(a, b))
            if engine == "scalar":
                nc.scalar.activation(pairs[g, t // 2][:, t % 2, a:b], window, ACT.Copy)
            else:
                nc.vector.tensor_copy(pairs[g, t // 2][:, t % 2, a:b], window)

        def gather_in_place(g, t, a, b):
            nc.vector.tensor_copy(grouped[g][:, a:b, t], raw[g, t][:].indirect(entries(a, b)))

        def place(g, u, a, b, copy=nc.vector.tensor_copy):
            copy(grouped[g][:, a:b, 2 * u : 2 * u + 2], pairs[g, u][:, :, a:b].rearrange("p t s -> p s t"))

        codes = [aligned([P, S], U32, name="codes%d" % g) for g in range(PASSES)]
        scales = [aligned([P, S], U8, name="scales%d" % g) for g in range(PASSES)]

        def quantise(g, a, b):
            nc.vector.quantize_mx(
                out=codes[g][:, a:b].bitcast(FP8X4),
                scales=scales[g][:, a:b],
                in_=grouped[g][:, a:b, :].rearrange("p s t -> p (s t)"),
            )

        last = PIECES - 1
        acc = {}
        for i in range(last):
            acc[i] = psum.tile([P, BLOCKS, PIECE], F32, name="acc%d" % i, tag="bank%d" % i)
        last_acc = [psum.tile([P, PIECE], F32, name="last%d" % b, tag="bank%d" % (6 + b)) for b in range(BLOCKS)]

        def products(g, i):
            tok = slice(i * PIECE, (i + 1) * PIECE)
            for b in range(BLOCKS):
                nc.tensor.matmul_mx(
                    out=last_acc[b][:] if i == last else acc[i][:, b, :],
                    lhsT=w_words[g][:, 2 * P * b : 2 * P * (b + 1)].bitcast(FP4X4),
                    lhsT_scale=w_scales[:, g, P * b : P * (b + 1)],
                    rhs=codes[g][:, tok].bitcast(FP8X4),
                    rhs_scale=scales[g][:, tok],
                    start=(g == 0 and (b == 0 or i == last)),
                    stop=(g == PASSES - 1 and (b == BLOCKS - 1 or i == last)),
                )

        half = S // 2
        grouped[0] = aligned([P, S, PACK], BF16, name="grouped0", tag="grouped")
        gather("vector", 0, 0, 0, S)
        gather("vector", 0, 1, 0, S)
        nc.scalar.activation(t_picked[:], t_window.indirect(offsets[:]), ACT.Copy)
        for t in (3, 2):
            gather("vector", 0, t, 0, half)
            gather("scalar", 0, t, half, S)
        for a in (0, half):
            nc.vector.tensor_copy(
                grouped[0][:, a : a + half, :].rearrange("p (c i) t -> p c t i", i=4),
                picked0[:, :, a : a + half].rearrange("p t (c i) -> p c t i", i=4),
            )
        quantise(0, 0, half)
        quantise(0, half, S)
        for i in range(PIECES):
            products(0, i)

        grouped[1] = aligned([P, S, PACK], BF16, name="grouped1", tag="grouped")
        picked1 = aligned([P, PACK, S], BF16, name="picked1", tag="raw0_2")
        pairs[1, 0] = picked1[:, 0:2, :]
        pairs[1, 1] = picked1[:, 2:4, :]
        gather("scalar", 1, 0, PIECE, S)
        gather("scalar", 1, 1, PIECE, S)
        for t in range(PACK - 1):
            gather_in_place(1, t, 0, PIECE)
        place(1, 0, PIECE, S)
        gather("scalar", 1, 2, PIECE, S)
        gather_in_place(1, 3, 0, PIECE)
        for i in range(1, PIECES):
            gather("scalar", 1, 3, i * PIECE, (i + 1) * PIECE)
        place(1, 1, PIECE, 2 * PIECE)
        for i in range(PIECES):
            quantise(1, i * PIECE, (i + 1) * PIECE)
            products(1, i)
            if i + 2 < PIECES:
                place(1, 1, (i + 2) * PIECE, (i + 3) * PIECE, nc.scalar.copy if i == 1 else nc.vector.tensor_copy)

        out_view = out.rearrange("(b p) s -> p b s", p=P)
        for i in range(last):
            tok = slice(i * PIECE, (i + 1) * PIECE)
            scaled = aligned([P, BLOCKS, PIECE], F32, name="scaled%d" % i)
            nc.vector.tensor_tensor(
                scaled[:], acc[i][:], t_picked[:, tok].unsqueeze(1).to_broadcast([P, BLOCKS, PIECE]), ALU.mult
            )
            result = aligned([P, BLOCKS, PIECE], F32, name="result%d" % i)
            for b in range(BLOCKS):
                nc.scalar.activation(result[:, b, :], scaled[:, b, :], ACT.Relu, scale=c_col[:, b : b + 1])
            nc.sync.dma_start(out=out_view[:, :, tok], in_=result[:])
        tok = slice(last * PIECE, S)
        for b in range(BLOCKS):
            scaled = aligned([P, PIECE], F32, name="last_scaled%d" % b)
            nc.vector.tensor_tensor(scaled[:], last_acc[b][:], t_picked[:, tok], ALU.mult)
            result = aligned([P, PIECE], F32, name="last_result%d" % b)
            nc.scalar.activation(result[:], scaled[:], ACT.Relu, scale=c_col[:, b : b + 1])
            nc.sync.dma_start(out=out_view[:, b, tok], in_=result[:])
